import numpy as np
import ml_dtypes


def mxq(x, axis, fmt="e4m3"):
    dtype, down = {"e4m3": (ml_dtypes.float8_e4m3fn, 7), "e5m2": (ml_dtypes.float8_e5m2, 14)}[fmt]
    v = np.moveaxis(np.asarray(x, np.float32).astype(ml_dtypes.bfloat16).astype(np.float64), axis, -1)
    blocks = v.reshape(v.shape[:-1] + (-1, 32))
    amax = np.abs(blocks).max(-1, keepdims=True)
    byte = np.maximum(np.where(amax > 0, np.frexp(amax)[1] - 1 + 127, 0) - down, 1)
    scale = np.exp2(byte - 127.0)
    codes = (blocks / scale).astype(np.float32).astype(dtype).astype(np.float64)
    return np.moveaxis((codes * scale).reshape(v.shape), -1, axis)


WIDE = False


def mx_kscale(k):
    if not WIDE:
        return np.ones(k)
    levels = np.array([10, -10, 5, -5, 0])
    if k % 512:
        return np.exp2(np.random.permutation(np.resize(levels, k // 32))).repeat(32)
    a = np.empty((k // 512, 16))
    for p in range(k // 512):
        a[p, :8] = np.random.permutation(np.resize(levels, 8))
        for g in range(8):
            far = levels[np.abs(levels - a[p, g]) >= 10]
            a[p, g + 8] = far[np.random.randint(len(far))]
    return np.exp2(a.ravel()).repeat(32)


def f64(x):
    return np.asarray(x).astype(np.float64)


def striped(idx):
    return np.tile(idx.reshape(-1, 16).T, (8, 1)).astype(np.uint16)


def unstriped(offs):
    return offs[:16].T.reshape(-1).astype(np.int64)


E2M1 = np.array([0.0, 0.5, 1.0, 1.5, 2.0, 3.0, 4.0, 6.0, -0.0, -0.5, -1.0, -1.5, -2.0, -3.0, -4.0, -6.0])


def pack_weight(w, fmt):
    k, n = w.shape
    w = f64(np.asarray(w, np.float32).astype(ml_dtypes.bfloat16)).reshape(k // 32, 32, n)
    amax = np.abs(w).max(1)
    if fmt == "e4m3":
        byte = np.frexp(amax)[1] - 1 + 127 - 7
    else:
        mant, ex = np.frexp(amax / 6.0)
        byte = np.where(mant > 0.5, ex, ex - 1) + 127
    byte = np.clip(np.where(amax > 0, byte, 1), 1, 254)
    scaled = (w * np.exp2(127.0 - byte)[:, None, :]).reshape(k, n).astype(np.float32)
    by_word = np.ascontiguousarray(scaled.reshape(k // 512, 128, 4, n).transpose(0, 1, 3, 2))
    if fmt == "e4m3":
        words = by_word.astype(ml_dtypes.float8_e4m3fn).view(np.uint8)
    else:
        c = by_word.astype(ml_dtypes.float4_e2m1fn).view(np.uint8) & 0xF
        words = (c[..., 0::2] | (c[..., 1::2] << 4)).reshape(k // 512, 128, 2 * n)
    return np.ascontiguousarray(words), np.ascontiguousarray(byte.astype(np.uint8).reshape(k // 512, 16, n))


def unpack_weight(words, scales, fmt):
    g, _, n = scales.shape
    words = np.ascontiguousarray(words).reshape(g, 128, n, -1)
    if fmt == "e4m3":
        vals = words.view(ml_dtypes.float8_e4m3fn).astype(np.float64)
    else:
        nib = np.empty((g, 128, n, 4), np.uint8)
        nib[..., 0::2] = words & 0xF
        nib[..., 1::2] = words >> 4
        vals = E2M1[nib]
    vals = vals * np.repeat(np.exp2(scales.astype(np.float64) - 127.0), 8, axis=1)[..., None]
    return vals.transpose(0, 1, 3, 2).reshape(g * 512, n)


def gelu(v):
    return 0.5 * v * (1.0 + np.tanh(np.sqrt(2.0 / np.pi) * (v + 0.044715 * v**3)))


K, K2, H, N, T, T2, S, P = 1024, 512, 1024, 384, 2048, 1024, 512, 512

def setup_inputs():
    n = np.random.standard_normal
    s = mx_kscale(K)[:, None]
    s2 = mx_kscale(K2)[:, None]
    u = mx_kscale(H)[:, None]
    tab_words, tab_scales = pack_weight(n((K, T)) * s, "e4m3")
    wa2_words, wa2_scales = pack_weight(n((K2, H)) / np.sqrt(K2) / s2, "e4m3")
    wb1_words, wb1_scales = pack_weight(n((K, H)) / np.sqrt(K) / s, "e2m1")
    return {
        "tab_words": tab_words, "tab_scales": tab_scales,
        "offs": striped(np.random.permutation(T)[:P]),
        "offs2": striped(np.random.permutation(T2)[:S]),
        "offs3": striped(np.random.permutation(T2)[:P]),
        "xs": (np.round(16 * n((K2, S))) / 16 * s2).astype(np.float32),
        "base": (n((K2, T2)) * s2).astype(np.float32),
        "wa1": (n((K2, H)) / np.sqrt(K2) / s2).astype(np.float32),
        "wa2_words": wa2_words, "wa2_scales": wa2_scales,
        "wb1_words": wb1_words, "wb1_scales": wb1_scales,
        "wb2": (n((K, H)) / np.sqrt(K) / s).astype(np.float32),
        "gain": (np.exp(0.3 * n(H)) * u[:, 0]).astype(np.float32),
        "wo": (2.0 * n((H, N)) / np.sqrt(H) / u).astype(np.float32),
    }

def reference(tab_words, tab_scales, offs, offs2, offs3, xs, base, wa1, wa2_words, wa2_scales, wb1_words, wb1_scales, wb2, gain, wo):
    v = unpack_weight(tab_words, tab_scales, "e4m3")[:, unstriped(offs)]
    page = f64(base).copy()
    page[:, unstriped(offs2)] = f64(xs)
    pq = mxq(page, 0, "e4m3")
    a1 = mxq(f64(wa1), 0, "e4m3").T @ pq
    a2 = unpack_weight(wa2_words, wa2_scales, "e4m3").T @ pq
    b1 = unpack_weight(wb1_words, wb1_scales, "e2m1").T @ v
    b2 = mxq(f64(wb2), 0, "e4m3").T @ v
    gate = 1.0 / (1.0 + np.exp(-(a1[:, unstriped(offs3)] + b1)))
    cand = np.tanh(a2[:, unstriped(offs3)] + b2)
    h = gate * cand * f64(gain)[:, None]
    return mxq(f64(wo), 0, "e4m3").T @ mxq(h, 0, "e4m3")

@@ -1,0 +1,504 @@
+from contextlib import ExitStack
+
+import concourse.mybir as mybir
+
+K, K2, H, N, T, T2, S, J = 1024, 512, 1024, 384, 2048, 1024, 512, 512
+FLOPS = 4697620480
+
+F32 = mybir.dt.float32
+BF16 = mybir.dt.bfloat16
+I32 = mybir.dt.int32
+U32 = mybir.dt.uint32
+U16 = mybir.dt.uint16
+U8 = mybir.dt.uint8
+FP8X4 = mybir.dt.float8_e4m3fn_x4
+FP4X4 = mybir.dt.float4_e2m1fn_x4
+ACT = mybir.ActivationFunctionType
+ALU = mybir.AluOpType
+
+P = 128
+FUSED = set()
+ENG = {("wa1",0,0):"S",("wb2",0,0):"S",("wb2",1,0):"S",("wa1",0,1):"S",("wb2",0,1):"S",("wb2",1,1):"S",
+ ("plane",0):"S",("plane",1):"S",("plane",2):"S",("plane",3):"S",("pweave",0):"V",("pweave",1):"S",
+ ("hweave",0,0):"S",("hweave",1,0):"S",("hweave",1,256):"V",("wo",0):"S",("wo",1):"S",
+ ("oev",0,0):"S",("oev",0,1):"S",("oev",0,2):"S",("oev",256,0):"S",("oev",256,1):"V",("oev",256,2):"S"}
+WARM = True
+
+
+def tile_list_intent_cell_step_kernel(
+    tc, tab_words, tab_scales, offs, offs2, offs3, xs, base, wa1, wa2_words, wa2_scales,
+    wb1_words, wb1_scales, wb2, gain, wo, out,
+):
+    nc = tc.nc
+
+    def copy(eng, dst, src):
+        if eng == "S":
+            nc.scalar.copy(dst, src)
+        elif eng == "V":
+            nc.vector.tensor_copy(dst, src)
+        else:
+            nc.gpsimd.tensor_scalar(dst, src, 1.0, 0.0, ALU.mult, ALU.add)
+
+    with ExitStack() as ctx:
+        keep = ctx.enter_context(tc.tile_pool(name="keep", bufs=1))
+        ring = ctx.enter_context(tc.tile_pool(name="ring", bufs=2))
+        psum = ctx.enter_context(tc.psum_pool(name="psum", bufs=4))
+
+        idx = keep.tile([P, J // 16], U16, name="idx")
+        idx2 = keep.tile([P, S // 16], U16, name="idx2")
+        idx3 = keep.tile([P, J // 16], U16, name="idx3")
+
+        tab_sc = keep.tile([P, 2, T], U8, name="tab_sc", align_bytes=64)
+        wa2_sc_raw = keep.tile([P, 1, H], U8, name="wa2_sc_raw", align_bytes=64)
+        wb1_sc_raw = keep.tile([P, 2, H], U8, name="wb1_sc_raw", align_bytes=64)
+        for tile in (wa2_sc_raw, tab_sc, wb1_sc_raw):
+            nc.vector.memset(tile[:].rearrange("p a c -> p (a c)").bitcast(I32), 0)
+        if WARM:
+            warm = keep.tile([P, 2], F32, name="warm")
+            nc.vector.memset(warm[:, 0:1], 0.0)
+            nc.scalar.activation(warm[:, 1:2], warm[:, 0:1], ACT.Sigmoid)
+        small = nc.sync
+
+        def load_scales(dst, src, q):
+            small.dma_start(
+                dst[32 * q : 32 * q + 4].bitcast(I32),
+                src[:, 4 * q : 4 * q + 4, :].rearrange("a r c -> r a c").bitcast(I32),
+            )
+
+        def scales_wa2():
+            for q in range(4):
+                load_scales(wa2_sc_raw[:], wa2_scales, q)
+
+        def scales_tab():
+            for q in range(4):
+                load_scales(tab_sc[:], tab_scales, q)
+
+        def scales_wb1():
+            for q in range(4):
+                load_scales(wb1_sc_raw[:], wb1_scales, q)
+
+        def clock(src, dt):
+            c = ring.tile([P, 1], dt, name="clk", tag="clk", bufs=8)
+            nc.gpsimd.tensor_copy(c[:], src)
+
+        base_v = base.rearrange("(p i) t -> i p t", i=4)
+        xs_v = xs.rearrange("(p i) t -> i p t", i=4)
+        page = [keep.tile([P, T2], F32, name=f"page{i}", tag=f"page{i}", align_bytes=64) for i in range(4)]
+        frames = [keep.tile([P, S], F32, name=f"frames{i}", tag=f"frames{i}", align_bytes=64) for i in range(4)]
+        raw = {}
+
+        def load_plane(i):
+            nc.sync.dma_start(page[i][:], base_v[i])
+            nc.sync.dma_start(frames[i][:], xs_v[i])
+
+        def load_weight(name, w, a, b):
+            t = ring.tile([P, 4, 512], F32, name=f"raw_{name}{a}{b}", tag="raw", bufs=4)
+            nc.sync.dma_start(
+                t[:], w[512 * a : 512 * (a + 1), 512 * b : 512 * (b + 1)].rearrange("(p i) c -> p i c", i=4)
+            )
+            raw[name, a, b] = t
+
+        tab_w = [keep.tile([P, T], I32, name=f"tab_w{a}", align_bytes=64) for a in range(2)]
+        wa2_raw = ring.tile([P, H], I32, name="wa2_raw", tag="a_full", bufs=8)
+        wb1_raw = ring.tile([P, 2, H // 2], I32, name="wb1_raw", tag="a_full", bufs=8)
+        wo_raw = {}
+        gain_sb = keep.tile([P, 2, 16], F32, name="gain_sb")
+
+        def load_tab(a):
+            nc.sync.dma_start(tab_w[a][:], tab_words[a].rearrange("p t i -> p (t i)").bitcast(I32))
+
+        def load_wa2():
+            nc.sync.dma_start(wa2_raw[:], wa2_words[0].rearrange("p c i -> p (c i)").bitcast(I32))
+
+        def load_wb1():
+            nc.sync.dma_start(wb1_raw[:], wb1_words.rearrange("a p c -> p a c").bitcast(I32))
+
+        def load_wo(b):
+            rows = wo[512 * b : 512 * (b + 1), :].rearrange("(g t e) n -> e g t n", t=4, e=4)
+            wo_raw[b] = ring.tile([P, 4, N], F32, name="wo_raw", tag="raw", bufs=4)
+            for e in range(4):
+                nc.sync.dma_start(wo_raw[b][e:P:4], rows[e])
+
+        def load_gain():
+            rows = gain.rearrange("(b g x) -> g b x", b=2, x=16)
+            for e in range(4):
+                nc.sync.dma_start(gain_sb[e:P:4, :, 0:13], rows[:, :, e : e + 13])
+
+        nc.sync.dma_start(idx2[:], offs2)
+        load_plane(0)
+        load_plane(1)
+        load_weight("wa1", wa1, 0, 0)
+        load_plane(2)
+        load_weight("wb2", wb2, 0, 0)
+        load_plane(3)
+        nc.sync.dma_start(idx[:], offs)
+        nc.sync.dma_start(idx3[:], offs3)
+        scales_wa2()
+        load_wa2()
+        scales_tab()
+        load_tab(0)
+        load_tab(1)
+        load_weight("wb2", wb2, 1, 0)
+        scales_wb1()
+        load_wb1()
+        load_weight("wa1", wa1, 0, 1)
+        load_gain()
+        load_weight("wb2", wb2, 0, 1)
+        load_weight("wb2", wb2, 1, 1)
+        load_wo(0)
+        load_wo(1)
+
+        def quantize(codes, scales, src):
+            nc.vector.quantize_mx(out=codes.bitcast(FP8X4), scales=scales, in_=src)
+
+        wq = {}
+
+        early = {}
+
+        def prep_weight(name, a, b):
+            eng = ENG[name, a, b]
+            src = raw[name, a, b]
+            grouped = ring.tile([P, 2048], BF16, name="grouped", tag="grouped", bufs=3, align_bytes=64)
+            dst_v = grouped[:].rearrange("p (t g e i) -> p t g i e", t=4, e=4, i=4)
+            src_v = src[:].rearrange("p i (g t e) -> p t g i e", t=4, e=4)
+            if eng == "G":
+                for t in range(4):
+                    copy(eng, dst_v[:, t], src_v[:, t])
+            else:
+                copy(eng, dst_v.rearrange("p t g i e -> p g t i e"), src_v.rearrange("p t g i e -> p g t i e"))
+            if (name, a, b) == ("wa1", 0, 0):
+                early["codes"] = keep.tile([P, 1024], U32, name="early_codes", tag="frames3", align_bytes=64)
+                codes = early["codes"][:, 0:512]
+            elif (name, a, b) == ("wb2", 0, 0):
+                codes = early["codes"][:, 512:1024]
+            else:
+                codes = keep.tile([P, 512], U32, name=f"{name}_codes{a}{b}", align_bytes=64)
+            scales = keep.tile([P, 512], U8, name=f"{name}_scales{a}{b}", align_bytes=64)
+            wq[name, a, b] = (codes, scales)
+            return lambda: quantize(codes[:], scales[:], grouped[:])
+
+        def weave(eng, dst, src, c0, c1):
+            copy(
+                eng,
+                dst[:, 4 * c0 : 4 * c1].rearrange("p (c e i) -> p c i e", e=4, i=4),
+                src[:, :, c0:c1].rearrange("p i (c e) -> p c i e", e=4),
+            )
+
+        page_bf = keep.tile([P, 4, T2], BF16, name="page_bf", tag="stage_a", align_bytes=64)
+        page_grp = [keep.tile([P, 2 * T2], BF16, name=f"page_grp{c}", tag=f"page_grp{c}", align_bytes=64) for c in range(2)]
+        page_codes = keep.tile([P, T2], U32, name="page_codes", align_bytes=64)
+        page_scales = keep.tile([P, T2], U8, name="page_scales", align_bytes=64)
+
+        def scatter(i):
+            nc.vector.tensor_copy(page[i][:].indirect(idx2[:]), frames[i][:])
+            if i < 3:
+                copy(ENG["plane", i], page_bf[:, i, :], page[i][:])
+
+        def last_plane(c):
+            copy(ENG["pweave", c], page_bf[:, 3, 512 * c : 512 * (c + 1)], page[3][:, 512 * c : 512 * (c + 1)])
+
+        def page_half(c):
+            weave(ENG["pweave", c], page_grp[c], page_bf[:, :, 512 * c : 512 * (c + 1)], 0, 512)
+
+        def page_quant(c):
+            quantize(page_codes[:, 512 * c : 512 * (c + 1)], page_scales[:, 512 * c : 512 * (c + 1)],
+                     page_grp[c][:])
+
+        wa2_codes = keep.tile([P, H], U32, name="wa2_codes", align_bytes=64)
+        late = {}
+        wa2_sc = keep.tile([P, H], U8, name="wa2_sc", align_bytes=64)
+        mover = nc.vector
+
+        def order_wa2():
+            mover.tensor_copy(
+                wa2_codes[:].bitcast(I32).rearrange("p (b t g e) -> p b t g e", b=2, t=4, e=4),
+                wa2_raw[:].rearrange("p (b g t e) -> p b t g e", b=2, t=4, e=4),
+            )
+            mover.tensor_copy(
+                wa2_sc[:].bitcast(I32).rearrange("p (b t g) -> p b t g", b=2, t=4),
+                wa2_sc_raw[:, 0, :].bitcast(I32).rearrange("p (b g t) -> p b t g", b=2, t=4),
+            )
+
+        def order_wb1():
+            wb1_codes = keep.tile([P, 2, 2 * H], U8, name="wb1_codes", tag="page_grp1", align_bytes=64)
+            late["wb1"] = wb1_codes
+            wb1_sc = keep.tile([P, 2, H], U8, name="wb1_sc", tag="page2", align_bytes=64)
+            late["wb1_sc"] = wb1_sc
+            mover.tensor_copy(
+                wb1_codes[:].rearrange("p a c -> p (a c)").bitcast(I32).rearrange("p (s t g w) -> p s t g w", s=4, t=4, w=2),
+                wb1_raw[:].rearrange("p a (b g t w) -> p (a b) t g w", b=2, t=4, w=2),
+            )
+            mover.tensor_copy(
+                wb1_sc[:].rearrange("p a c -> p (a c)").bitcast(I32).rearrange("p (s t g) -> p s t g", s=4, t=4),
+                wb1_sc_raw[:].rearrange("p a c -> p (a c)").bitcast(I32).rearrange("p (s g t) -> p s t g", s=4, t=4),
+            )
+
+        v_codes = {}
+        v_scales = {}
+
+        def open_table():
+            codes = keep.tile([P, 2 * J], U32, name="v_codes", tag="page_grp0", align_bytes=64)
+            scales = keep.tile([P, 2 * J], U8, name="v_scales", tag="page3", align_bytes=64)
+            for a in range(2):
+                v_codes[a] = codes[:, J * a : J * (a + 1)]
+                v_scales[a] = scales[:, J * a : J * (a + 1)]
+
+        def gather_words(a):
+            nc.vector.tensor_copy(v_codes[a], tab_w[a][:].bitcast(U32).indirect(idx[:]))
+
+        def gather_scales(a):
+            nc.vector.tensor_copy(v_scales[a], tab_sc[:, a, :].indirect(idx[:]))
+
+        a_sb = {}
+
+        def project_page(b, t):
+            for which in (1, 2):
+                if which == 1:
+                    codes, scales = wq["wa1", 0, b]
+                    cols = slice(128 * t, 128 * (t + 1))
+                else:
+                    codes, scales = wa2_codes, wa2_sc
+                    cols = slice(512 * b + 128 * t, 512 * b + 128 * (t + 1))
+                full = ring.tile([P, T2], F32, name="a_full", tag="a_full", bufs=8)
+                for c in range(2):
+                    half = slice(512 * c, 512 * (c + 1))
+                    bank = psum.tile([P, 512], F32, name="bank_a", tag="bank_a")
+                    nc.tensor.matmul_mx(
+                        out=bank[:], lhsT=codes[:, cols].bitcast(FP8X4), lhsT_scale=scales[:, cols],
+                        rhs=page_codes[:, half].bitcast(FP8X4), rhs_scale=page_scales[:, half],
+                        start=True, stop=True,
+                    )
+                    copy(ENG.get(("aev", b, t, which, c), "S"), full[:, half], bank[:])
+                a_sb[which, b, t] = full
+
+        steps = [(0, (0,), 0, 512), (0, (1,), 0, 512), (0, (2,), 0, 512), (0, (3,), 0, 512),
+                 (1, (0,), 0, 512), (1, (1,), 0, 512), (1, (2, 3), 0, 256), (1, (2, 3), 256, 256)]
+        b_src = {}
+        sums = {}
+        acts = {}
+
+        def project_states(s):
+            b, ts, j0, w = steps[s]
+            for which in (1, 2):
+                bank = psum.tile([P, 512], F32, name="bank_b", tag="bank_b")
+                n = w if (which == 2 or w == 512) else 128
+                for k, t in enumerate(ts):
+                    for c0 in range(0, w, n):
+                        for a in range(2):
+                            if which == 1:
+                                col = 512 * b + 128 * t
+                                lhs = late["wb1"][:, a, 2 * col : 2 * col + 256].bitcast(FP4X4)
+                                lhs_sc = late["wb1_sc"][:, a, col : col + 128]
+                            else:
+                                codes, scales = wq["wb2", a, b]
+                                lhs = codes[:, 128 * t : 128 * (t + 1)].bitcast(FP8X4)
+                                lhs_sc = scales[:, 128 * t : 128 * (t + 1)]
+                            js = slice(j0 + c0, j0 + c0 + n)
+                            nc.tensor.matmul_mx(
+                                out=bank[:, k * w + c0 : k * w + c0 + n], lhsT=lhs, lhsT_scale=lhs_sc,
+                                rhs=v_codes[a][:, js].bitcast(FP8X4), rhs_scale=v_scales[a][:, js],
+                                start=(a == 0), stop=(a == 1),
+                            )
+                if (s, which) in FUSED:
+                    b_sb = ring.tile([P, 512], F32, name="b_sb", tag="b_sb", bufs=4)
+                    nc.scalar.copy(b_sb[:], bank[:])
+                    b_src[s, which] = b_sb
+                else:
+                    b_src[s, which] = bank
+
+        picked = {}
+
+        def gather_page(s, which):
+            b, ts, j0, w = steps[s]
+            offsets = idx3[:, j0 // 16 : (j0 + w) // 16]
+            if (s, which) in FUSED:
+                total = ring.tile([P, 512], F32, name="total", tag="total", bufs=4)
+                for k, t in enumerate(ts):
+                    cols = slice(k * w, (k + 1) * w)
+                    nc.vector.tensor_tensor(
+                        total[:, cols], a_sb[which, b, t][:].indirect(offsets), b_src[s, which][:, cols], ALU.add)
+                sums[s, which] = total
+            else:
+                got = ring.tile([P, 512], F32, name="got", tag="got", bufs=3)
+                for k, t in enumerate(ts):
+                    nc.vector.tensor_copy(got[:, k * w : (k + 1) * w], a_sb[which, b, t][:].indirect(offsets))
+                picked[s, which] = got
+
+        def add_states(s, which):
+            if (s, which) not in FUSED:
+                total = ring.tile([P, 512], F32, name="total", tag="total", bufs=4)
+                nc.vector.tensor_tensor(total[:], b_src[s, which][:], picked[s, which][:], ALU.add)
+                sums[s, which] = total
+
+        def activate(s, which):
+            res = ring.tile([P, 512], F32, name="act", tag="act", bufs=4)
+            nc.scalar.activation(res[:], sums[s, which][:], ACT.Sigmoid if which == 1 else ACT.Tanh)
+            acts[s, which] = res
+
+        hb = {}
+
+        def open_h():
+            h_bf_all = keep.tile([P, 8, J], BF16, name="h_bf", tag="stage_b", align_bytes=64)
+            h_grp_all = keep.tile([P, 8 * J], BF16, name="h_grp", tag="stage_a", align_bytes=64)
+            for b in range(2):
+                hb["bf", b] = h_bf_all[:, 4 * b : 4 * (b + 1), :]
+                hb["grp", b] = h_grp_all[:, 4 * J * b : 4 * J * (b + 1)]
+
+        h_codes = [keep.tile([P, J], U32, name=f"h_codes{b}", align_bytes=64) for b in range(2)]
+        h_scales = [keep.tile([P, J], U8, name=f"h_scales{b}", align_bytes=64) for b in range(2)]
+
+        def product(s):
+            b, ts, j0, w = steps[s]
+            for k, t in enumerate(ts):
+                cols = slice(k * w, (k + 1) * w)
+                nc.vector.scalar_tensor_tensor(
+                    hb["bf", b][:, t, j0 : j0 + w], acts[s, 1][:, cols], gain_sb[:, b, 4 * t : 4 * t + 1],
+                    acts[s, 2][:, cols], ALU.mult, ALU.mult)
+
+        def h_weave(b, j0, w):
+            weave(ENG["hweave", b, j0], hb["grp", b], hb["bf", b], j0, j0 + w)
+
+        def h_quant(b, j0, w):
+            quantize(h_codes[b][:, j0 : j0 + w], h_scales[b][:, j0 : j0 + w], hb["grp", b][:, 4 * j0 : 4 * (j0 + w)])
+
+        wo_grp = keep.tile([P, 2 * 4 * N], BF16, name="wo_grp", align_bytes=64)
+        wo_codes = keep.tile([P, 2 * N], U32, name="wo_codes", align_bytes=64)
+        wo_scales = keep.tile([P, 2 * N], U8, name="wo_scales", align_bytes=64)
+
+        def wo_weave(b):
+            weave(ENG["wo", b], wo_grp[:, 4 * N * b : 4 * N * (b + 1)], wo_raw[b], 0, N)
+
+        def wo_quant():
+            quantize(wo_codes[:, 0:512], wo_scales[:, 0:512], wo_grp[:, 0:2048])
+            quantize(wo_codes[:, 512:768], wo_scales[:, 512:768], wo_grp[:, 2048:3072])
+
+        out_v = out.rearrange("(m p) j -> p m j", p=P)
+
+        def finish(j0, w):
+            js = slice(j0, j0 + w)
+            res = ring.tile([P, 3, w], F32, name="res", tag="res", bufs=2)
+            for m in range(3):
+                bank = psum.tile([P, w], F32, name="bank_o", tag="bank_a")
+                for b in range(2):
+                    cols = slice(N * b + 128 * m, N * b + 128 * (m + 1))
+                    nc.tensor.matmul_mx(
+                        out=bank[:], lhsT=wo_codes[:, cols].bitcast(FP8X4), lhsT_scale=wo_scales[:, cols],
+                        rhs=h_codes[b][:, js].bitcast(FP8X4), rhs_scale=h_scales[b][:, js],
+                        start=(b == 0), stop=(b == 1),
+                    )
+                copy(ENG["oev", j0, m], res[:, m, :], bank[:])
+            nc.sync.dma_start(out_v[:, :, js], res[:])
+
+        scatter(0)
+        scatter(1)
+        q_wa1 = prep_weight("wa1", 0, 0)
+        scatter(2)
+        scatter(3)
+        q_wb2a = prep_weight("wb2", 0, 0)
+        last_plane(0)
+        last_plane(1)
+        q_wa1()
+        page_half(0)
+        page_half(1)
+        order_wa2()
+        page_quant(0)
+        open_table()
+        gather_scales(0)
+        page_quant(1)
+        q_wb2b = prep_weight("wb2", 1, 0)
+        gather_words(0)
+        gather_words(1)
+        gather_scales(1)
+        q_wb2a()
+        project_page(0, 0)
+        order_wb1()
+        q_wb2b()
+        project_page(0, 1)
+        project_states(0)
+        gather_page(0, 1)
+        gather_page(0, 2)
+        add_states(0, 1)
+        add_states(0, 2)
+        project_page(0, 2)
+        q1 = prep_weight("wa1", 0, 1)
+        project_states(1)
+        gather_page(1, 1)
+        q1()
+        gather_page(1, 2)
+        add_states(1, 1)
+        add_states(1, 2)
+        activate(0, 1)
+        activate(0, 2)
+        project_page(0, 3)
+        q2 = prep_weight("wb2", 0, 1)
+        project_states(2)
+        gather_page(2, 1)
+        open_h()
+        product(0)
+        gather_page(2, 2)
+        q2()
+        add_states(2, 1)
+        add_states(2, 2)
+        activate(1, 1)
+        activate(1, 2)
+        q3 = prep_weight("wb2", 1, 1)
+        project_page(1, 0)
+        project_states(3)
+        gather_page(3, 1)
+        product(1)
+        gather_page(3, 2)
+        q3()
+        add_states(3, 1)
+        add_states(3, 2)
+        activate(2, 1)
+        activate(2, 2)
+        project_page(1, 1)
+        project_states(4)
+        gather_page(4, 1)
+        product(2)
+        gather_page(4, 2)
+        add_states(4, 1)
+        add_states(4, 2)
+        activate(3, 1)
+        activate(3, 2)
+        project_page(1, 2)
+        project_states(5)
+        gather_page(5, 1)
+        product(3)
+        gather_page(5, 2)
+        add_states(5, 1)
+        add_states(5, 2)
+        project_page(1, 3)
+        activate(4, 1)
+        activate(4, 2)
+        h_weave(0, 0, 512)
+        project_states(6)
+        gather_page(6, 1)
+        product(4)
+        gather_page(6, 2)
+        add_states(6, 1)
+        add_states(6, 2)
+        activate(5, 1)
+        activate(5, 2)
+        wo_weave(0)
+        wo_weave(1)
+        h_quant(0, 0, 512)
+        project_states(7)
+        gather_page(7, 1)
+        product(5)
+        add_states(7, 1)
+        activate(6, 1)
+        activate(6, 2)
+        gather_page(7, 2)
+        product(6)
+        wo_quant()
+        add_states(7, 2)
+        h_weave(1, 0, 256)
+        activate(7, 1)
+        activate(7, 2)
+        h_quant(1, 0, 256)
+        product(7)
+        finish(0, 256)
+        h_weave(1, 256, 256)
+        h_quant(1, 256, 256)
+        finish(256, 256)

@@ -17,10 +17,10 @@ ACT = mybir.ActivationFunctionType
 ALU = mybir.AluOpType
 
 P = 128
-FUSED = set()
-ENG = {("wa1",0,0):"S",("wb2",0,0):"S",("wb2",1,0):"S",("wa1",0,1):"S",("wb2",0,1):"S",("wb2",1,1):"S",
+FUSED = {(s, w) for s in range(8) for w in (1, 2)}
+ENG = {("wa1",0,0):"S",("wb2",0,0):"S",("wb2",1,0):"S",("wa1",0,1):"V",("wb2",0,1):"V",("wb2",1,1):"V",
  ("plane",0):"S",("plane",1):"S",("plane",2):"S",("plane",3):"S",("pweave",0):"V",("pweave",1):"S",
- ("hweave",0,0):"S",("hweave",1,0):"S",("hweave",1,256):"V",("wo",0):"S",("wo",1):"S",
+ ("hweave",0,0):"V",("hweave",1,0):"S",("hweave",1,256):"V",("wo",0):"V",("wo",1):"S",
  ("oev",0,0):"S",("oev",0,1):"S",("oev",0,2):"S",("oev",256,0):"S",("oev",256,1):"V",("oev",256,2):"S"}
 WARM = True
 
@@ -415,86 +415,71 @@ def tile_list_intent_cell_step_kernel(
         q_wb2b()
         project_page(0, 1)
         project_states(0)
-        gather_page(0, 1)
-        gather_page(0, 2)
-        add_states(0, 1)
-        add_states(0, 2)
-        project_page(0, 2)
         q1 = prep_weight("wa1", 0, 1)
+        project_page(0, 2)
         project_states(1)
-        gather_page(1, 1)
+        gather_page(0, 1)
         q1()
-        gather_page(1, 2)
-        add_states(1, 1)
-        add_states(1, 2)
+        gather_page(0, 2)
+        q2 = prep_weight("wb2", 0, 1)
         activate(0, 1)
         activate(0, 2)
         project_page(0, 3)
-        q2 = prep_weight("wb2", 0, 1)
         project_states(2)
-        gather_page(2, 1)
+        gather_page(1, 1)
+        q2()
+        gather_page(1, 2)
+        q3 = prep_weight("wb2", 1, 1)
+        open_h()
         open_h()
         product(0)
-        gather_page(2, 2)
-        q2()
-        add_states(2, 1)
-        add_states(2, 2)
         activate(1, 1)
         activate(1, 2)
-        q3 = prep_weight("wb2", 1, 1)
         project_page(1, 0)
         project_states(3)
-        gather_page(3, 1)
-        product(1)
-        gather_page(3, 2)
+        gather_page(2, 1)
         q3()
-        add_states(3, 1)
-        add_states(3, 2)
+        gather_page(2, 2)
+        product(1)
         activate(2, 1)
         activate(2, 2)
         project_page(1, 1)
         project_states(4)
-        gather_page(4, 1)
+        gather_page(3, 1)
+        wo_weave(0)
+        gather_page(3, 2)
         product(2)
-        gather_page(4, 2)
-        add_states(4, 1)
-        add_states(4, 2)
         activate(3, 1)
         activate(3, 2)
         project_page(1, 2)
         project_states(5)
-        gather_page(5, 1)
+        gather_page(4, 1)
         product(3)
-        gather_page(5, 2)
-        add_states(5, 1)
-        add_states(5, 2)
-        project_page(1, 3)
+        gather_page(4, 2)
+        h_weave(0, 0, 512)
         activate(4, 1)
         activate(4, 2)
-        h_weave(0, 0, 512)
+        project_page(1, 3)
         project_states(6)
-        gather_page(6, 1)
+        gather_page(5, 1)
+        h_quant(0, 0, 512)
+        gather_page(5, 2)
         product(4)
-        gather_page(6, 2)
-        add_states(6, 1)
-        add_states(6, 2)
         activate(5, 1)
         activate(5, 2)
-        wo_weave(0)
-        wo_weave(1)
-        h_quant(0, 0, 512)
         project_states(7)
-        gather_page(7, 1)
+        wo_weave(1)
+        gather_page(6, 1)
+        gather_page(6, 2)
         product(5)
-        add_states(7, 1)
+        wo_quant()
         activate(6, 1)
         activate(6, 2)
-        gather_page(7, 2)
+        gather_page(7, 1)
         product(6)
-        wo_quant()
-        add_states(7, 2)
-        h_weave(1, 0, 256)
         activate(7, 1)
+        h_weave(1, 0, 256)
+        gather_page(7, 2)
         activate(7, 2)
         h_quant(1, 0, 256)
         product(7)

@@ -2,7 +2,7 @@ from contextlib import ExitStack
 
 import concourse.mybir as mybir
 
-K, K2, H, N, T, T2, S, J = 1024, 512, 1024, 384, 2048, 1024, 512, 512
+H, N, T, T2, S, J = 1024, 384, 2048, 1024, 512, 512
 FLOPS = 4697620480
 
 F32 = mybir.dt.float32
@@ -17,12 +17,12 @@ ACT = mybir.ActivationFunctionType
 ALU = mybir.AluOpType
 
 P = 128
-FUSED = {(s, w) for s in range(8) for w in (1, 2)}
-ENG = {("wa1",0,0):"S",("wb2",0,0):"S",("wb2",1,0):"S",("wa1",0,1):"V",("wb2",0,1):"V",("wb2",1,1):"V",
- ("plane",0):"S",("plane",1):"S",("plane",2):"S",("plane",3):"S",("pweave",0):"V",("pweave",1):"S",
- ("hweave",0,0):"V",("hweave",1,0):"S",("hweave",1,256):"V",("wo",0):"V",("wo",1):"S",
- ("oev",0,0):"S",("oev",0,1):"S",("oev",0,2):"S",("oev",256,0):"S",("oev",256,1):"V",("oev",256,2):"S"}
-WARM = True
+PASS = 512
+BANK = 512
+GATE, CAND = 0, 1
+ROW_TILES = [(b, t) for b in range(2) for t in range(4)]
+AHEAD = 3
+HALF = J // 2
 
 
 def tile_list_intent_cell_step_kernel(
@@ -30,460 +30,350 @@ def tile_list_intent_cell_step_kernel(
     wb1_words, wb1_scales, wb2, gain, wo, out,
 ):
     nc = tc.nc
-
-    def copy(eng, dst, src):
-        if eng == "S":
-            nc.scalar.copy(dst, src)
-        elif eng == "V":
-            nc.vector.tensor_copy(dst, src)
-        else:
-            nc.gpsimd.tensor_scalar(dst, src, 1.0, 0.0, ALU.mult, ALU.add)
+    on_scalar = nc.scalar.copy
+    on_vector = nc.vector.tensor_copy
 
     with ExitStack() as ctx:
         keep = ctx.enter_context(tc.tile_pool(name="keep", bufs=1))
         ring = ctx.enter_context(tc.tile_pool(name="ring", bufs=2))
-        psum = ctx.enter_context(tc.psum_pool(name="psum", bufs=4))
+        psum = ctx.enter_context(tc.psum_pool(name="psum", bufs=8))
 
         idx = keep.tile([P, J // 16], U16, name="idx")
         idx2 = keep.tile([P, S // 16], U16, name="idx2")
         idx3 = keep.tile([P, J // 16], U16, name="idx3")
 
-        tab_sc = keep.tile([P, 2, T], U8, name="tab_sc", align_bytes=64)
+        tab_sc = keep.tile([P, 2, T], U8, name="tab_sc", tag="tab_sc", align_bytes=64)
         wa2_sc_raw = keep.tile([P, 1, H], U8, name="wa2_sc_raw", align_bytes=64)
-        wb1_sc_raw = keep.tile([P, 2, H], U8, name="wb1_sc_raw", align_bytes=64)
-        for tile in (wa2_sc_raw, tab_sc, wb1_sc_raw):
-            nc.vector.memset(tile[:].rearrange("p a c -> p (a c)").bitcast(I32), 0)
-        if WARM:
-            warm = keep.tile([P, 2], F32, name="warm")
-            nc.vector.memset(warm[:, 0:1], 0.0)
-            nc.scalar.activation(warm[:, 1:2], warm[:, 0:1], ACT.Sigmoid)
-        small = nc.sync
+        wb1_sc_raw = keep.tile([P, 2, H], U8, name="wb1_sc_raw", tag="wb1_sc_raw", align_bytes=64)
+        for plane in (wa2_sc_raw, tab_sc, wb1_sc_raw):
+            nc.vector.memset(plane[:].rearrange("p a c -> p (a c)").bitcast(I32), 0)
 
-        def load_scales(dst, src, q):
-            small.dma_start(
-                dst[32 * q : 32 * q + 4].bitcast(I32),
-                src[:, 4 * q : 4 * q + 4, :].rearrange("a r c -> r a c").bitcast(I32),
-            )
+        def load_scales(plane, src):
+            for quad in range(4):
+                nc.sync.dma_start(
+                    plane[32 * quad : 32 * quad + 4].bitcast(I32),
+                    src[:, 4 * quad : 4 * quad + 4, :].rearrange("a r c -> r a c").bitcast(I32),
+                )
 
-        def scales_wa2():
-            for q in range(4):
-                load_scales(wa2_sc_raw[:], wa2_scales, q)
-
-        def scales_tab():
-            for q in range(4):
-                load_scales(tab_sc[:], tab_scales, q)
-
-        def scales_wb1():
-            for q in range(4):
-                load_scales(wb1_sc_raw[:], wb1_scales, q)
-
-        def clock(src, dt):
-            c = ring.tile([P, 1], dt, name="clk", tag="clk", bufs=8)
-            nc.gpsimd.tensor_copy(c[:], src)
-
-        base_v = base.rearrange("(p i) t -> i p t", i=4)
-        xs_v = xs.rearrange("(p i) t -> i p t", i=4)
-        page = [keep.tile([P, T2], F32, name=f"page{i}", tag=f"page{i}", align_bytes=64) for i in range(4)]
+        base_rows = base.rearrange("(p i) t -> i p t", i=4)
+        xs_rows = xs.rearrange("(p i) t -> i p t", i=4)
+        page = [keep.tile([P, T2], F32, name=f"page{i}", align_bytes=64) for i in range(4)]
         frames = [keep.tile([P, S], F32, name=f"frames{i}", tag=f"frames{i}", align_bytes=64) for i in range(4)]
+
+        def load_page_rows(i):
+            nc.sync.dma_start(page[i][:], base_rows[i])
+            nc.sync.dma_start(frames[i][:], xs_rows[i])
+
         raw = {}
 
-        def load_plane(i):
-            nc.sync.dma_start(page[i][:], base_v[i])
-            nc.sync.dma_start(frames[i][:], xs_v[i])
+        def streamed(columns):
+            return ring.tile([P, 4, columns], F32, name="raw", tag="raw", bufs=4)
 
-        def load_weight(name, w, a, b):
-            t = ring.tile([P, 4, 512], F32, name=f"raw_{name}{a}{b}", tag="raw", bufs=4)
-            nc.sync.dma_start(
-                t[:], w[512 * a : 512 * (a + 1), 512 * b : 512 * (b + 1)].rearrange("(p i) c -> p i c", i=4)
-            )
-            raw[name, a, b] = t
-
-        tab_w = [keep.tile([P, T], I32, name=f"tab_w{a}", align_bytes=64) for a in range(2)]
-        wa2_raw = ring.tile([P, H], I32, name="wa2_raw", tag="a_full", bufs=8)
-        wb1_raw = ring.tile([P, 2, H // 2], I32, name="wb1_raw", tag="a_full", bufs=8)
-        wo_raw = {}
-        gain_sb = keep.tile([P, 2, 16], F32, name="gain_sb")
-
-        def load_tab(a):
-            nc.sync.dma_start(tab_w[a][:], tab_words[a].rearrange("p t i -> p (t i)").bitcast(I32))
-
-        def load_wa2():
-            nc.sync.dma_start(wa2_raw[:], wa2_words[0].rearrange("p c i -> p (c i)").bitcast(I32))
-
-        def load_wb1():
-            nc.sync.dma_start(wb1_raw[:], wb1_words.rearrange("a p c -> p a c").bitcast(I32))
+        def load_weight(name, w, a, b, dst):
+            rows = w[PASS * a : PASS * (a + 1), PASS * b : PASS * (b + 1)]
+            raw[name, a, b] = dst
+            nc.sync.dma_start(dst[:], rows.rearrange("(p i) c -> p i c", i=4))
 
         def load_wo(b):
-            rows = wo[512 * b : 512 * (b + 1), :].rearrange("(g t e) n -> e g t n", t=4, e=4)
-            wo_raw[b] = ring.tile([P, 4, N], F32, name="wo_raw", tag="raw", bufs=4)
+            rows = wo[PASS * b : PASS * (b + 1), :].rearrange("(g t e) n -> e g t n", t=4, e=4)
+            raw["wo", b] = streamed(N)
             for e in range(4):
-                nc.sync.dma_start(wo_raw[b][e:P:4], rows[e])
+                nc.sync.dma_start(raw["wo", b][e:P:4], rows[e])
+
+        tab_w = [keep.tile([P, T], I32, name=f"tab_w{a}", tag=f"tab_w{a}", align_bytes=64) for a in range(2)]
+        wa2_raw = keep.tile([P, H], I32, name="wa2_raw")
+        wb1_raw = keep.tile([P, 2, H // 2], I32, name="wb1_raw", tag="wb1_raw", align_bytes=64)
+
+        gain_sb = keep.tile([P, 2, 16], F32, name="gain_sb")
 
         def load_gain():
-            rows = gain.rearrange("(b g x) -> g b x", b=2, x=16)
+            runs = gain.rearrange("(b g x) -> g b x", b=2, x=16)
             for e in range(4):
-                nc.sync.dma_start(gain_sb[e:P:4, :, 0:13], rows[:, :, e : e + 13])
-
-        nc.sync.dma_start(idx2[:], offs2)
-        load_plane(0)
-        load_plane(1)
-        load_weight("wa1", wa1, 0, 0)
-        load_plane(2)
-        load_weight("wb2", wb2, 0, 0)
-        load_plane(3)
-        nc.sync.dma_start(idx[:], offs)
-        nc.sync.dma_start(idx3[:], offs3)
-        scales_wa2()
-        load_wa2()
-        scales_tab()
-        load_tab(0)
-        load_tab(1)
-        load_weight("wb2", wb2, 1, 0)
-        scales_wb1()
-        load_wb1()
-        load_weight("wa1", wa1, 0, 1)
-        load_gain()
-        load_weight("wb2", wb2, 0, 1)
-        load_weight("wb2", wb2, 1, 1)
-        load_wo(0)
-        load_wo(1)
+                nc.sync.dma_start(gain_sb[e:P:4, :, 0:13], runs[:, :, e : e + 13])
 
         def quantize(codes, scales, src):
             nc.vector.quantize_mx(out=codes.bitcast(FP8X4), scales=scales, in_=src)
 
-        wq = {}
+        def weave(copy, dst, src):
+            copy(dst.rearrange("p (c e i) -> p c i e", e=4, i=4), src.rearrange("p i (c e) -> p c i e", e=4))
 
-        early = {}
+        woven = {}
+        quantized = {}
 
-        def prep_weight(name, a, b):
-            eng = ENG[name, a, b]
-            src = raw[name, a, b]
-            grouped = ring.tile([P, 2048], BF16, name="grouped", tag="grouped", bufs=3, align_bytes=64)
-            dst_v = grouped[:].rearrange("p (t g e i) -> p t g i e", t=4, e=4, i=4)
-            src_v = src[:].rearrange("p i (g t e) -> p t g i e", t=4, e=4)
-            if eng == "G":
-                for t in range(4):
-                    copy(eng, dst_v[:, t], src_v[:, t])
+        def round_weight(copy, name, a, b, after=None):
+            if after is None:
+                dst = ring.tile([P, 4 * PASS], BF16, name="woven", tag="woven", bufs=3, align_bytes=64)
             else:
-                copy(eng, dst_v.rearrange("p t g i e -> p g t i e"), src_v.rearrange("p t g i e -> p g t i e"))
-            if (name, a, b) == ("wa1", 0, 0):
-                early["codes"] = keep.tile([P, 1024], U32, name="early_codes", tag="frames3", align_bytes=64)
-                codes = early["codes"][:, 0:512]
-            elif (name, a, b) == ("wb2", 0, 0):
-                codes = early["codes"][:, 512:1024]
-            else:
-                codes = keep.tile([P, 512], U32, name=f"{name}_codes{a}{b}", align_bytes=64)
-            scales = keep.tile([P, 512], U8, name=f"{name}_scales{a}{b}", align_bytes=64)
-            wq[name, a, b] = (codes, scales)
-            return lambda: quantize(codes[:], scales[:], grouped[:])
-
-        def weave(eng, dst, src, c0, c1):
+                dst = keep.tile([P, 4 * PASS], BF16, name="woven_late", tag=after, align_bytes=64)
             copy(
-                eng,
-                dst[:, 4 * c0 : 4 * c1].rearrange("p (c e i) -> p c i e", e=4, i=4),
-                src[:, :, c0:c1].rearrange("p i (c e) -> p c i e", e=4),
+                dst[:].rearrange("p (t g e i) -> p g t i e", t=4, e=4, i=4),
+                raw[name, a, b][:].rearrange("p i (g t e) -> p g t i e", t=4, e=4),
             )
+            woven[name, a, b] = dst
 
-        page_bf = keep.tile([P, 4, T2], BF16, name="page_bf", tag="stage_a", align_bytes=64)
-        page_grp = [keep.tile([P, 2 * T2], BF16, name=f"page_grp{c}", tag=f"page_grp{c}", align_bytes=64) for c in range(2)]
+        def quantize_weight(name, a, b, after=""):
+            codes = keep.tile([P, PASS], U32, name=f"{name}_codes{a}{b}", tag=after, align_bytes=64)
+            scales = keep.tile([P, PASS], U8, name=f"{name}_scales{a}{b}", align_bytes=64)
+            quantize(codes[:], scales[:], woven[name, a, b][:])
+            quantized[name, a, b] = (codes, scales)
+
+        page_woven = [
+            keep.tile([P, 4 * BANK], BF16, name=f"page_woven{c}", tag=f"page_woven{c}", align_bytes=64)
+            for c in range(2)
+        ]
         page_codes = keep.tile([P, T2], U32, name="page_codes", align_bytes=64)
         page_scales = keep.tile([P, T2], U8, name="page_scales", align_bytes=64)
 
         def scatter(i):
             nc.vector.tensor_copy(page[i][:].indirect(idx2[:]), frames[i][:])
-            if i < 3:
-                copy(ENG["plane", i], page_bf[:, i, :], page[i][:])
 
-        def last_plane(c):
-            copy(ENG["pweave", c], page_bf[:, 3, 512 * c : 512 * (c + 1)], page[3][:, 512 * c : 512 * (c + 1)])
-
-        def page_half(c):
-            weave(ENG["pweave", c], page_grp[c], page_bf[:, :, 512 * c : 512 * (c + 1)], 0, 512)
-
-        def page_quant(c):
-            quantize(page_codes[:, 512 * c : 512 * (c + 1)], page_scales[:, 512 * c : 512 * (c + 1)],
-                     page_grp[c][:])
+        def quantize_page(c):
+            cols = slice(BANK * c, BANK * (c + 1))
+            quantize(page_codes[:, cols], page_scales[:, cols], page_woven[c][:])
 
         wa2_codes = keep.tile([P, H], U32, name="wa2_codes", align_bytes=64)
-        late = {}
         wa2_sc = keep.tile([P, H], U8, name="wa2_sc", align_bytes=64)
-        mover = nc.vector
 
-        def order_wa2():
-            mover.tensor_copy(
+        def order_wa2_words():
+            nc.vector.tensor_copy(
                 wa2_codes[:].bitcast(I32).rearrange("p (b t g e) -> p b t g e", b=2, t=4, e=4),
                 wa2_raw[:].rearrange("p (b g t e) -> p b t g e", b=2, t=4, e=4),
             )
-            mover.tensor_copy(
+
+        def order_wa2_scales():
+            nc.vector.tensor_copy(
                 wa2_sc[:].bitcast(I32).rearrange("p (b t g) -> p b t g", b=2, t=4),
                 wa2_sc_raw[:, 0, :].bitcast(I32).rearrange("p (b g t) -> p b t g", b=2, t=4),
             )
 
         def order_wb1():
-            wb1_codes = keep.tile([P, 2, 2 * H], U8, name="wb1_codes", tag="page_grp1", align_bytes=64)
-            late["wb1"] = wb1_codes
-            wb1_sc = keep.tile([P, 2, H], U8, name="wb1_sc", tag="page2", align_bytes=64)
-            late["wb1_sc"] = wb1_sc
-            mover.tensor_copy(
-                wb1_codes[:].rearrange("p a c -> p (a c)").bitcast(I32).rearrange("p (s t g w) -> p s t g w", s=4, t=4, w=2),
+            codes = keep.tile([P, 2, 2 * H], U8, name="wb1_codes", tag="tab_w1", align_bytes=64)
+            scales = keep.tile([P, 2, H], U8, name="wb1_sc", tag="tab_sc", align_bytes=64)
+            as_words = "p a c -> p (a c)"
+            nc.vector.tensor_copy(
+                codes[:].rearrange(as_words).bitcast(I32).rearrange("p (u t g w) -> p u t g w", u=4, t=4, w=2),
                 wb1_raw[:].rearrange("p a (b g t w) -> p (a b) t g w", b=2, t=4, w=2),
             )
-            mover.tensor_copy(
-                wb1_sc[:].rearrange("p a c -> p (a c)").bitcast(I32).rearrange("p (s t g) -> p s t g", s=4, t=4),
-                wb1_sc_raw[:].rearrange("p a c -> p (a c)").bitcast(I32).rearrange("p (s g t) -> p s t g", s=4, t=4),
+            nc.vector.tensor_copy(
+                scales[:].rearrange(as_words).bitcast(I32).rearrange("p (u t g) -> p u t g", u=4, t=4),
+                wb1_sc_raw[:].rearrange(as_words).bitcast(I32).rearrange("p (u g t) -> p u t g", u=4, t=4),
             )
+            return codes, scales
 
-        v_codes = {}
-        v_scales = {}
-
-        def open_table():
-            codes = keep.tile([P, 2 * J], U32, name="v_codes", tag="page_grp0", align_bytes=64)
-            scales = keep.tile([P, 2 * J], U8, name="v_scales", tag="page3", align_bytes=64)
+        def gather_table():
+            codes = keep.tile([P, 2 * J], U32, name="v_codes", tag="page_woven1", align_bytes=64)
             for a in range(2):
-                v_codes[a] = codes[:, J * a : J * (a + 1)]
-                v_scales[a] = scales[:, J * a : J * (a + 1)]
+                nc.vector.tensor_copy(codes[:, J * a : J * (a + 1)], tab_w[a][:].bitcast(U32).indirect(idx[:]))
+            scales = keep.tile([P, 2 * J], U8, name="v_scales", tag="tab_w0", align_bytes=64)
+            for a in range(2):
+                nc.vector.tensor_copy(scales[:, J * a : J * (a + 1)], tab_sc[:, a, :].indirect(idx[:]))
+            return codes, scales
 
-        def gather_words(a):
-            nc.vector.tensor_copy(v_codes[a], tab_w[a][:].bitcast(U32).indirect(idx[:]))
+        with tc.tile_pool(name="staging", bufs=1) as staging:
+            stretch = 2 * 4 * PASS
+            stage = staging.tile([P, 4 * stretch + BANK], BF16, name="stage", align_bytes=64)
+            page_rows = stage[:, 0 : 4 * stretch].rearrange("p (i c) -> p i c", i=4)[:, :, 0:T2]
 
-        def gather_scales(a):
-            nc.vector.tensor_copy(v_scales[a], tab_sc[:, a, :].indirect(idx[:]))
+            def staged(start):
+                return stage[:, start : start + stretch].bitcast(F32).rearrange("p (i c) -> p i c", i=4)
+
+            nc.sync.dma_start(idx2[:], offs2)
+            load_page_rows(0)
+            load_page_rows(1)
+            load_weight("wa1", wa1, 0, 0, staged(stretch))
+            load_page_rows(2)
+            load_weight("wb2", wb2, 0, 0, staged(2 * stretch))
+            load_page_rows(3)
+            load_weight("wb2", wb2, 1, 0, staged(3 * stretch + BANK))
+            load_scales(wa2_sc_raw, wa2_scales)
+            nc.sync.dma_start(wa2_raw[:], wa2_words[0].rearrange("p c i -> p (c i)").bitcast(I32))
+            nc.sync.dma_start(idx[:], offs)
+            load_scales(tab_sc, tab_scales)
+            for a in range(2):
+                nc.sync.dma_start(tab_w[a][:], tab_words[a].rearrange("p t i -> p (t i)").bitcast(I32))
+            nc.sync.dma_start(idx3[:], offs3)
+            load_scales(wb1_sc_raw, wb1_scales)
+            nc.sync.dma_start(wb1_raw[:], wb1_words.rearrange("a p c -> p a c").bitcast(I32))
+            load_weight("wa1", wa1, 0, 1, streamed(PASS))
+            load_weight("wb2", wb2, 0, 1, streamed(PASS))
+            load_gain()
+            load_weight("wb2", wb2, 1, 1, streamed(PASS))
+            load_wo(0)
+            load_wo(1)
+
+            for i, piece in enumerate((("wa1", 0, 0), ("wb2", 0, 0), ("wb2", 1, 0))):
+                scatter(i)
+                on_scalar(page_rows[:, i, :], page[i][:])
+                round_weight(on_scalar, *piece)
+            scatter(3)
+            halves = ((on_vector, slice(0, BANK)), (on_scalar, slice(BANK, T2)))
+            for copy, cols in halves:
+                copy(page_rows[:, 3, cols], page[3][:, cols])
+            quantize_weight("wa1", 0, 0, after="frames3")
+            for c, (copy, cols) in enumerate(halves):
+                weave(copy, page_woven[c][:], page_rows[:, :, cols])
+
+        products = ctx.enter_context(tc.tile_pool(name="products", bufs=2 * (AHEAD + 1)))
+
+        order_wa2_scales()
+        quantize_page(0)
+        order_wa2_words()
+        quantize_weight("wb2", 0, 0, after="page_woven0")
+        quantize_page(1)
+        quantize_weight("wb2", 1, 0)
+        v_codes, v_scales = gather_table()
+        wb1_codes, wb1_sc = order_wb1()
 
         a_sb = {}
-
-        def project_page(b, t):
-            for which in (1, 2):
-                if which == 1:
-                    codes, scales = wq["wa1", 0, b]
-                    cols = slice(128 * t, 128 * (t + 1))
-                else:
-                    codes, scales = wa2_codes, wa2_sc
-                    cols = slice(512 * b + 128 * t, 512 * b + 128 * (t + 1))
-                full = ring.tile([P, T2], F32, name="a_full", tag="a_full", bufs=8)
-                for c in range(2):
-                    half = slice(512 * c, 512 * (c + 1))
-                    bank = psum.tile([P, 512], F32, name="bank_a", tag="bank_a")
-                    nc.tensor.matmul_mx(
-                        out=bank[:], lhsT=codes[:, cols].bitcast(FP8X4), lhsT_scale=scales[:, cols],
-                        rhs=page_codes[:, half].bitcast(FP8X4), rhs_scale=page_scales[:, half],
-                        start=True, stop=True,
-                    )
-                    copy(ENG.get(("aev", b, t, which, c), "S"), full[:, half], bank[:])
-                a_sb[which, b, t] = full
-
-        steps = [(0, (0,), 0, 512), (0, (1,), 0, 512), (0, (2,), 0, 512), (0, (3,), 0, 512),
-                 (1, (0,), 0, 512), (1, (1,), 0, 512), (1, (2, 3), 0, 256), (1, (2, 3), 256, 256)]
-        b_src = {}
+        b_sb = {}
         sums = {}
         acts = {}
 
-        def project_states(s):
-            b, ts, j0, w = steps[s]
-            for which in (1, 2):
-                bank = psum.tile([P, 512], F32, name="bank_b", tag="bank_b")
-                n = w if (which == 2 or w == 512) else 128
-                for k, t in enumerate(ts):
-                    for c0 in range(0, w, n):
-                        for a in range(2):
-                            if which == 1:
-                                col = 512 * b + 128 * t
-                                lhs = late["wb1"][:, a, 2 * col : 2 * col + 256].bitcast(FP4X4)
-                                lhs_sc = late["wb1_sc"][:, a, col : col + 128]
-                            else:
-                                codes, scales = wq["wb2", a, b]
-                                lhs = codes[:, 128 * t : 128 * (t + 1)].bitcast(FP8X4)
-                                lhs_sc = scales[:, 128 * t : 128 * (t + 1)]
-                            js = slice(j0 + c0, j0 + c0 + n)
-                            nc.tensor.matmul_mx(
-                                out=bank[:, k * w + c0 : k * w + c0 + n], lhsT=lhs, lhsT_scale=lhs_sc,
-                                rhs=v_codes[a][:, js].bitcast(FP8X4), rhs_scale=v_scales[a][:, js],
-                                start=(a == 0), stop=(a == 1),
-                            )
-                if (s, which) in FUSED:
-                    b_sb = ring.tile([P, 512], F32, name="b_sb", tag="b_sb", bufs=4)
-                    nc.scalar.copy(b_sb[:], bank[:])
-                    b_src[s, which] = b_sb
+        def project_page(b, t):
+            for branch in (GATE, CAND):
+                if branch == GATE:
+                    codes, scales = quantized["wa1", 0, b]
+                    rows = slice(P * t, P * (t + 1))
                 else:
-                    b_src[s, which] = bank
+                    codes, scales = wa2_codes, wa2_sc
+                    rows = slice(PASS * b + P * t, PASS * b + P * (t + 1))
+                full = products.tile([P, T2], F32, name="a_full")
+                for c in range(2):
+                    cols = slice(BANK * c, BANK * (c + 1))
+                    bank = psum.tile([P, BANK], F32, name="bank_a", tag="bank")
+                    nc.tensor.matmul_mx(
+                        out=bank[:], lhsT=codes[:, rows].bitcast(FP8X4), lhsT_scale=scales[:, rows],
+                        rhs=page_codes[:, cols].bitcast(FP8X4), rhs_scale=page_scales[:, cols],
+                        start=True, stop=True,
+                    )
+                    on_scalar(full[:, cols], bank[:])
+                a_sb[branch, b, t] = full
 
-        picked = {}
+        def project_states(b, t):
+            for branch in (GATE, CAND):
+                bank = psum.tile([P, BANK], F32, name="bank_b", tag="bank")
+                for a in range(2):
+                    if branch == GATE:
+                        first = PASS * b + P * t
+                        lhs = wb1_codes[:, a, 2 * first : 2 * (first + P)].bitcast(FP4X4)
+                        lhs_scale = wb1_sc[:, a, first : first + P]
+                    else:
+                        codes, scales = quantized["wb2", a, b]
+                        lhs = codes[:, P * t : P * (t + 1)].bitcast(FP8X4)
+                        lhs_scale = scales[:, P * t : P * (t + 1)]
+                    picked = slice(J * a, J * (a + 1))
+                    nc.tensor.matmul_mx(
+                        out=bank[:], lhsT=lhs, lhsT_scale=lhs_scale,
+                        rhs=v_codes[:, picked].bitcast(FP8X4), rhs_scale=v_scales[:, picked],
+                        start=(a == 0), stop=(a == 1),
+                    )
+                b_sb[branch, b, t] = ring.tile([P, J], F32, name="b_sb", tag="b_sb", bufs=6)
+                on_scalar(b_sb[branch, b, t][:], bank[:])
 
-        def gather_page(s, which):
-            b, ts, j0, w = steps[s]
-            offsets = idx3[:, j0 // 16 : (j0 + w) // 16]
-            if (s, which) in FUSED:
-                total = ring.tile([P, 512], F32, name="total", tag="total", bufs=4)
-                for k, t in enumerate(ts):
-                    cols = slice(k * w, (k + 1) * w)
-                    nc.vector.tensor_tensor(
-                        total[:, cols], a_sb[which, b, t][:].indirect(offsets), b_src[s, which][:, cols], ALU.add)
-                sums[s, which] = total
-            else:
-                got = ring.tile([P, 512], F32, name="got", tag="got", bufs=3)
-                for k, t in enumerate(ts):
-                    nc.vector.tensor_copy(got[:, k * w : (k + 1) * w], a_sb[which, b, t][:].indirect(offsets))
-                picked[s, which] = got
+        def gather_add(branch, b, t, j0, width):
+            total = ring.tile([P, width], F32, name="total", tag="total", bufs=4)
+            nc.vector.tensor_tensor(
+                total[:], a_sb[branch, b, t][:].indirect(idx3[:, j0 // 16 : (j0 + width) // 16]),
+                b_sb[branch, b, t][:, j0 : j0 + width], ALU.add,
+            )
+            sums[branch, b, t, j0] = total
 
-        def add_states(s, which):
-            if (s, which) not in FUSED:
-                total = ring.tile([P, 512], F32, name="total", tag="total", bufs=4)
-                nc.vector.tensor_tensor(total[:], b_src[s, which][:], picked[s, which][:], ALU.add)
-                sums[s, which] = total
+        def activate(branch, b, t, j0, width):
+            value = ring.tile([P, width], F32, name="act", tag="act", bufs=4)
+            nc.scalar.activation(value[:], sums[branch, b, t, j0][:], ACT.Sigmoid if branch == GATE else ACT.Tanh)
+            acts[branch, b, t, j0] = value
 
-        def activate(s, which):
-            res = ring.tile([P, 512], F32, name="act", tag="act", bufs=4)
-            nc.scalar.activation(res[:], sums[s, which][:], ACT.Sigmoid if which == 1 else ACT.Tanh)
-            acts[s, which] = res
-
-        hb = {}
-
-        def open_h():
-            h_bf_all = keep.tile([P, 8, J], BF16, name="h_bf", tag="stage_b", align_bytes=64)
-            h_grp_all = keep.tile([P, 8 * J], BF16, name="h_grp", tag="stage_a", align_bytes=64)
-            for b in range(2):
-                hb["bf", b] = h_bf_all[:, 4 * b : 4 * (b + 1), :]
-                hb["grp", b] = h_grp_all[:, 4 * J * b : 4 * J * (b + 1)]
-
+        h_stage = keep.tile([P, 16 * J], BF16, name="h_stage", align_bytes=64)
+        h_woven = h_stage[:, 0 : 8 * J]
+        h_rows = h_stage[:, 8 * J : 16 * J].rearrange("p (u j) -> p u j", j=J)
         h_codes = [keep.tile([P, J], U32, name=f"h_codes{b}", align_bytes=64) for b in range(2)]
         h_scales = [keep.tile([P, J], U8, name=f"h_scales{b}", align_bytes=64) for b in range(2)]
 
-        def product(s):
-            b, ts, j0, w = steps[s]
-            for k, t in enumerate(ts):
-                cols = slice(k * w, (k + 1) * w)
-                nc.vector.scalar_tensor_tensor(
-                    hb["bf", b][:, t, j0 : j0 + w], acts[s, 1][:, cols], gain_sb[:, b, 4 * t : 4 * t + 1],
-                    acts[s, 2][:, cols], ALU.mult, ALU.mult)
+        def product(b, t, j0, width):
+            nc.vector.scalar_tensor_tensor(
+                h_rows[:, 4 * b + t, j0 : j0 + width], acts[GATE, b, t, j0][:], gain_sb[:, b, 4 * t : 4 * t + 1],
+                acts[CAND, b, t, j0][:], ALU.mult, ALU.mult,
+            )
 
-        def h_weave(b, j0, w):
-            weave(ENG["hweave", b, j0], hb["grp", b], hb["bf", b], j0, j0 + w)
+        def weave_h(copy, b, j0, width):
+            start = 4 * (J * b + j0)
+            weave(copy, h_woven[:, start : start + 4 * width], h_rows[:, 4 * b : 4 * (b + 1), j0 : j0 + width])
 
-        def h_quant(b, j0, w):
-            quantize(h_codes[b][:, j0 : j0 + w], h_scales[b][:, j0 : j0 + w], hb["grp", b][:, 4 * j0 : 4 * (j0 + w)])
+        def quantize_h(b, j0, width):
+            start = 4 * (J * b + j0)
+            cols = slice(j0, j0 + width)
+            quantize(h_codes[b][:, cols], h_scales[b][:, cols], h_woven[:, start : start + 4 * width])
 
-        wo_grp = keep.tile([P, 2 * 4 * N], BF16, name="wo_grp", align_bytes=64)
+        wo_woven = keep.tile([P, 2 * 4 * N], BF16, name="wo_woven", tag="page_woven0", align_bytes=64)
         wo_codes = keep.tile([P, 2 * N], U32, name="wo_codes", align_bytes=64)
         wo_scales = keep.tile([P, 2 * N], U8, name="wo_scales", align_bytes=64)
 
-        def wo_weave(b):
-            weave(ENG["wo", b], wo_grp[:, 4 * N * b : 4 * N * (b + 1)], wo_raw[b], 0, N)
+        def round_wo(b):
+            weave(on_vector, wo_woven[:, 4 * N * b : 4 * N * (b + 1)], raw["wo", b][:])
 
-        def wo_quant():
-            quantize(wo_codes[:, 0:512], wo_scales[:, 0:512], wo_grp[:, 0:2048])
-            quantize(wo_codes[:, 512:768], wo_scales[:, 512:768], wo_grp[:, 2048:3072])
+        def quantize_wo():
+            for cols in (slice(0, 512), slice(512, 2 * N)):
+                quantize(wo_codes[:, cols], wo_scales[:, cols], wo_woven[:, 4 * cols.start : 4 * cols.stop])
 
-        out_v = out.rearrange("(m p) j -> p m j", p=P)
-
-        def finish(j0, w):
-            js = slice(j0, j0 + w)
-            res = ring.tile([P, 3, w], F32, name="res", tag="res", bufs=2)
-            for m in range(3):
-                bank = psum.tile([P, w], F32, name="bank_o", tag="bank_a")
+        def finish(j0, copies):
+            cols = slice(j0, j0 + HALF)
+            for m in range(N // P):
+                bank = psum.tile([P, HALF], F32, name="bank_out", tag="bank")
                 for b in range(2):
-                    cols = slice(N * b + 128 * m, N * b + 128 * (m + 1))
+                    rows = slice(N * b + P * m, N * b + P * (m + 1))
                     nc.tensor.matmul_mx(
-                        out=bank[:], lhsT=wo_codes[:, cols].bitcast(FP8X4), lhsT_scale=wo_scales[:, cols],
-                        rhs=h_codes[b][:, js].bitcast(FP8X4), rhs_scale=h_scales[b][:, js],
+                        out=bank[:], lhsT=wo_codes[:, rows].bitcast(FP8X4), lhsT_scale=wo_scales[:, rows],
+                        rhs=h_codes[b][:, cols].bitcast(FP8X4), rhs_scale=h_scales[b][:, cols],
                         start=(b == 0), stop=(b == 1),
                     )
-                copy(ENG["oev", j0, m], res[:, m, :], bank[:])
-            nc.sync.dma_start(out_v[:, :, js], res[:])
+                result = ring.tile([P, HALF], F32, name="result", tag="result", bufs=6)
+                copies[m](result[:], bank[:])
+                nc.sync.dma_start(out[P * m : P * (m + 1), cols], result[:])
 
-        scatter(0)
-        scatter(1)
-        q_wa1 = prep_weight("wa1", 0, 0)
-        scatter(2)
-        scatter(3)
-        q_wb2a = prep_weight("wb2", 0, 0)
-        last_plane(0)
-        last_plane(1)
-        q_wa1()
-        page_half(0)
-        page_half(1)
-        order_wa2()
-        page_quant(0)
-        open_table()
-        gather_scales(0)
-        page_quant(1)
-        q_wb2b = prep_weight("wb2", 1, 0)
-        gather_words(0)
-        gather_words(1)
-        gather_scales(1)
-        q_wb2a()
-        project_page(0, 0)
-        order_wb1()
-        q_wb2b()
-        project_page(0, 1)
-        project_states(0)
-        q1 = prep_weight("wa1", 0, 1)
-        project_page(0, 2)
-        project_states(1)
-        gather_page(0, 1)
-        q1()
-        gather_page(0, 2)
-        q2 = prep_weight("wb2", 0, 1)
-        activate(0, 1)
-        activate(0, 2)
-        project_page(0, 3)
-        project_states(2)
-        gather_page(1, 1)
-        q2()
-        gather_page(1, 2)
-        q3 = prep_weight("wb2", 1, 1)
-        open_h()
-        open_h()
-        product(0)
-        activate(1, 1)
-        activate(1, 2)
-        project_page(1, 0)
-        project_states(3)
-        gather_page(2, 1)
-        q3()
-        gather_page(2, 2)
-        product(1)
-        activate(2, 1)
-        activate(2, 2)
-        project_page(1, 1)
-        project_states(4)
-        gather_page(3, 1)
-        wo_weave(0)
-        gather_page(3, 2)
-        product(2)
-        activate(3, 1)
-        activate(3, 2)
-        project_page(1, 2)
-        project_states(5)
-        gather_page(4, 1)
-        product(3)
-        gather_page(4, 2)
-        h_weave(0, 0, 512)
-        activate(4, 1)
-        activate(4, 2)
-        project_page(1, 3)
-        project_states(6)
-        gather_page(5, 1)
-        h_quant(0, 0, 512)
-        gather_page(5, 2)
-        product(4)
-        activate(5, 1)
-        activate(5, 2)
-        project_states(7)
-        wo_weave(1)
-        gather_page(6, 1)
-        gather_page(6, 2)
-        product(5)
-        wo_quant()
-        activate(6, 1)
-        activate(6, 2)
-        gather_page(7, 1)
-        product(6)
-        activate(7, 1)
-        h_weave(1, 0, 256)
-        gather_page(7, 2)
-        activate(7, 2)
-        h_quant(1, 0, 256)
-        product(7)
-        finish(0, 256)
-        h_weave(1, 256, 256)
-        h_quant(1, 256, 256)
-        finish(256, 256)
+        for tile in ROW_TILES[:AHEAD]:
+            project_page(*tile)
+        project_states(*ROW_TILES[0])
+        round_weight(on_vector, "wa1", 0, 1, after="wb1_raw")
+        quantize_weight("wa1", 0, 1)
+
+        side_work = {
+            1: (lambda: round_weight(on_vector, "wb2", 0, 1, after="wb1_sc_raw"), lambda: quantize_weight("wb2", 0, 1)),
+            2: (lambda: round_weight(on_vector, "wb2", 1, 1, after="wb1_sc_raw"), lambda: quantize_weight("wb2", 1, 1)),
+            4: (lambda: round_wo(0), lambda: None),
+            5: (lambda: weave_h(on_vector, 0, 0, J), lambda: quantize_h(0, 0, J)),
+        }
+        whole_tiles = ROW_TILES[:-2]
+        for step, tile in enumerate(whole_tiles):
+            before, after = side_work.get(step, (lambda: None, lambda: None))
+            before()
+            gather_add(GATE, *tile, 0, J)
+            after()
+            project_states(*ROW_TILES[step + 1])
+            if step + AHEAD < len(ROW_TILES):
+                project_page(*ROW_TILES[step + AHEAD])
+            gather_add(CAND, *tile, 0, J)
+            if step > 0:
+                product(*whole_tiles[step - 1], 0, J)
+            activate(GATE, *tile, 0, J)
+            activate(CAND, *tile, 0, J)
+        project_states(*ROW_TILES[-1])
+
+        pieces = [(b, t, j0, HALF) for j0 in (0, HALF) for b, t in ROW_TILES[-2:]]
+        pending = whole_tiles[-1] + (0, J)
+        for n, piece in enumerate(pieces):
+            for branch in (GATE, CAND):
+                gather_add(branch, *piece)
+                activate(branch, *piece)
+            product(*pending)
+            pending = piece
+            if n == 0:
+                round_wo(1)
+                quantize_wo()
+            if n == 2:
+                weave_h(on_scalar, 1, 0, HALF)
+        quantize_h(1, 0, HALF)
+        product(*pending)
+        finish(0, (on_scalar, on_scalar, on_scalar))
+        weave_h(on_vector, 1, HALF, HALF)
+        quantize_h(1, HALF, HALF)
+        finish(HALF, (on_scalar, on_vector, on_scalar))

@@ -44,9 +44,13 @@ def tile_list_intent_cell_step_kernel(
 
         tab_sc = keep.tile([P, 2, T], U8, name="tab_sc", tag="tab_sc", align_bytes=64)
         wa2_sc_raw = keep.tile([P, 1, H], U8, name="wa2_sc_raw", align_bytes=64)
-        wb1_sc_raw = keep.tile([P, 2, H], U8, name="wb1_sc_raw", tag="wb1_sc_raw", align_bytes=64)
+        wb1_sc_raw = keep.tile([P, 2, H], U8, name="wb1_sc_raw", align_bytes=64)
         for plane in (wa2_sc_raw, tab_sc, wb1_sc_raw):
             nc.vector.memset(plane[:].rearrange("p a c -> p (a c)").bitcast(I32), 0)
+
+        warm = keep.tile([P, 2], F32, name="warm")
+        nc.vector.memset(warm[:, 0:1], 0.0)
+        nc.scalar.activation(warm[:, 1:2], warm[:, 0:1], ACT.Sigmoid)
 
         def load_scales(plane, src):
             for quad in range(4):
@@ -267,7 +271,10 @@ def tile_list_intent_cell_step_kernel(
                         rhs=v_codes[:, picked].bitcast(FP8X4), rhs_scale=v_scales[:, picked],
                         start=(a == 0), stop=(a == 1),
                     )
-                b_sb[branch, b, t] = ring.tile([P, J], F32, name="b_sb", tag="b_sb", bufs=6)
+                if branch == GATE and (b, t) in ROW_TILES[:2]:
+                    b_sb[branch, b, t] = keep.tile([P, J], F32, name="b_first", tag=f"b_first{t}", align_bytes=64)
+                else:
+                    b_sb[branch, b, t] = ring.tile([P, J], F32, name="b_sb", tag="b_sb", bufs=6)
                 on_scalar(b_sb[branch, b, t][:], bank[:])
 
         def gather_add(branch, b, t, j0, width):
@@ -308,8 +315,8 @@ def tile_list_intent_cell_step_kernel(
         wo_codes = keep.tile([P, 2 * N], U32, name="wo_codes", align_bytes=64)
         wo_scales = keep.tile([P, 2 * N], U8, name="wo_scales", align_bytes=64)
 
-        def round_wo(b):
-            weave(on_vector, wo_woven[:, 4 * N * b : 4 * N * (b + 1)], raw["wo", b][:])
+        def round_wo(copy, b):
+            weave(copy, wo_woven[:, 4 * N * b : 4 * N * (b + 1)], raw["wo", b][:])
 
         def quantize_wo():
             for cols in (slice(0, 512), slice(512, 2 * N)):
@@ -334,12 +341,12 @@ def tile_list_intent_cell_step_kernel(
             project_page(*tile)
         project_states(*ROW_TILES[0])
         round_weight(on_vector, "wa1", 0, 1, after="wb1_raw")
-        quantize_weight("wa1", 0, 1)
 
         side_work = {
-            1: (lambda: round_weight(on_vector, "wb2", 0, 1, after="wb1_sc_raw"), lambda: quantize_weight("wb2", 0, 1)),
-            2: (lambda: round_weight(on_vector, "wb2", 1, 1, after="wb1_sc_raw"), lambda: quantize_weight("wb2", 1, 1)),
-            4: (lambda: round_wo(0), lambda: None),
+            0: (lambda: None, lambda: quantize_weight("wa1", 0, 1)),
+            1: (lambda: round_weight(on_vector, "wb2", 0, 1, after="b_first0"), lambda: quantize_weight("wb2", 0, 1)),
+            2: (lambda: round_weight(on_vector, "wb2", 1, 1, after="b_first1"), lambda: quantize_weight("wb2", 1, 1)),
+            4: (lambda: round_wo(on_vector, 0), lambda: None),
             5: (lambda: weave_h(on_vector, 0, 0, J), lambda: quantize_h(0, 0, J)),
         }
         whole_tiles = ROW_TILES[:-2]
@@ -367,7 +374,8 @@ def tile_list_intent_cell_step_kernel(
             product(*pending)
             pending = piece
             if n == 0:
-                round_wo(1)
+                round_wo(on_scalar, 1)
+            if n == 1:
                 quantize_wo()
             if n == 2:
                 weave_h(on_scalar, 1, 0, HALF)

@@ -33,6 +33,13 @@ def tile_list_intent_cell_step_kernel(
     on_scalar = nc.scalar.copy
     on_vector = nc.vector.tensor_copy
 
+    def on_gpsimd(dst, src):
+        for t in range(4):
+            nc.gpsimd.tensor_scalar(
+                dst[:, :, t].rearrange("p g i e -> p g e i"), src[:, :, t].rearrange("p g i e -> p g e i"),
+                1.0, 0.0, ALU.mult, ALU.add,
+            )
+
     with ExitStack() as ctx:
         keep = ctx.enter_context(tc.tile_pool(name="keep", bufs=1))
         ring = ctx.enter_context(tc.tile_pool(name="ring", bufs=2))
@@ -44,7 +51,7 @@ def tile_list_intent_cell_step_kernel(
 
         tab_sc = keep.tile([P, 2, T], U8, name="tab_sc", tag="tab_sc", align_bytes=64)
         wa2_sc_raw = keep.tile([P, 1, H], U8, name="wa2_sc_raw", align_bytes=64)
-        wb1_sc_raw = keep.tile([P, 2, H], U8, name="wb1_sc_raw", align_bytes=64)
+        wb1_sc_raw = keep.tile([P, 2, H], U8, name="wb1_sc_raw", tag="wb1_sc_raw", align_bytes=64)
         for plane in (wa2_sc_raw, tab_sc, wb1_sc_raw):
             nc.vector.memset(plane[:].rearrange("p a c -> p (a c)").bitcast(I32), 0)
 
@@ -85,6 +92,10 @@ def tile_list_intent_cell_step_kernel(
                 nc.sync.dma_start(raw["wo", b][e:P:4], rows[e])
 
         tab_w = [keep.tile([P, T], I32, name=f"tab_w{a}", tag=f"tab_w{a}", align_bytes=64) for a in range(2)]
+
+        def load_table_words(a):
+            nc.sync.dma_start(tab_w[a][:], tab_words[a].rearrange("p t i -> p (t i)").bitcast(I32))
+
         wa2_raw = keep.tile([P, H], I32, name="wa2_raw")
         wb1_raw = keep.tile([P, 2, H // 2], I32, name="wb1_raw", tag="wb1_raw", align_bytes=64)
 
@@ -104,19 +115,16 @@ def tile_list_intent_cell_step_kernel(
         woven = {}
         quantized = {}
 
-        def round_weight(copy, name, a, b, after=None):
-            if after is None:
-                dst = ring.tile([P, 4 * PASS], BF16, name="woven", tag="woven", bufs=3, align_bytes=64)
-            else:
-                dst = keep.tile([P, 4 * PASS], BF16, name="woven_late", tag=after, align_bytes=64)
+        def round_weight(copy, name, a, b, on_bytes_of=None):
+            dst = keep.tile([P, 4 * PASS], BF16, name="woven", tag=on_bytes_of or f"woven_{name}{a}{b}", align_bytes=64)
             copy(
                 dst[:].rearrange("p (t g e i) -> p g t i e", t=4, e=4, i=4),
                 raw[name, a, b][:].rearrange("p i (g t e) -> p g t i e", t=4, e=4),
             )
             woven[name, a, b] = dst
 
-        def quantize_weight(name, a, b, after=""):
-            codes = keep.tile([P, PASS], U32, name=f"{name}_codes{a}{b}", tag=after, align_bytes=64)
+        def quantize_weight(name, a, b, on_bytes_of=""):
+            codes = keep.tile([P, PASS], U32, name=f"{name}_codes{a}{b}", tag=on_bytes_of, align_bytes=64)
             scales = keep.tile([P, PASS], U8, name=f"{name}_scales{a}{b}", align_bytes=64)
             quantize(codes[:], scales[:], woven[name, a, b][:])
             quantized[name, a, b] = (codes, scales)
@@ -193,27 +201,27 @@ def tile_list_intent_cell_step_kernel(
             nc.sync.dma_start(wa2_raw[:], wa2_words[0].rearrange("p c i -> p (c i)").bitcast(I32))
             nc.sync.dma_start(idx[:], offs)
             load_scales(tab_sc, tab_scales)
-            for a in range(2):
-                nc.sync.dma_start(tab_w[a][:], tab_words[a].rearrange("p t i -> p (t i)").bitcast(I32))
+            load_table_words(0)
+            load_weight("wa1", wa1, 0, 1, streamed(PASS))
+            load_table_words(1)
             nc.sync.dma_start(idx3[:], offs3)
             load_scales(wb1_sc_raw, wb1_scales)
             nc.sync.dma_start(wb1_raw[:], wb1_words.rearrange("a p c -> p a c").bitcast(I32))
-            load_weight("wa1", wa1, 0, 1, streamed(PASS))
             load_weight("wb2", wb2, 0, 1, streamed(PASS))
             load_gain()
             load_weight("wb2", wb2, 1, 1, streamed(PASS))
             load_wo(0)
             load_wo(1)
 
-            for i, piece in enumerate((("wa1", 0, 0), ("wb2", 0, 0), ("wb2", 1, 0))):
+            for i, weight_piece in enumerate((("wa1", 0, 0), ("wb2", 0, 0), ("wb2", 1, 0))):
                 scatter(i)
                 on_scalar(page_rows[:, i, :], page[i][:])
-                round_weight(on_scalar, *piece)
+                round_weight(on_scalar, *weight_piece)
             scatter(3)
             halves = ((on_vector, slice(0, BANK)), (on_scalar, slice(BANK, T2)))
             for copy, cols in halves:
                 copy(page_rows[:, 3, cols], page[3][:, cols])
-            quantize_weight("wa1", 0, 0, after="frames3")
+            quantize_weight("wa1", 0, 0, on_bytes_of="frames3")
             for c, (copy, cols) in enumerate(halves):
                 weave(copy, page_woven[c][:], page_rows[:, :, cols])
 
@@ -222,9 +230,10 @@ def tile_list_intent_cell_step_kernel(
         order_wa2_scales()
         quantize_page(0)
         order_wa2_words()
-        quantize_weight("wb2", 0, 0, after="page_woven0")
+        quantize_weight("wb2", 0, 0, on_bytes_of="page_woven0")
         quantize_page(1)
         quantize_weight("wb2", 1, 0)
+        round_weight(on_gpsimd, "wa1", 0, 1, on_bytes_of="woven_wb210")
         v_codes, v_scales = gather_table()
         wb1_codes, wb1_sc = order_wb1()
 
@@ -271,8 +280,8 @@ def tile_list_intent_cell_step_kernel(
                         rhs=v_codes[:, picked].bitcast(FP8X4), rhs_scale=v_scales[:, picked],
                         start=(a == 0), stop=(a == 1),
                     )
-                if branch == GATE and (b, t) in ROW_TILES[:2]:
-                    b_sb[branch, b, t] = keep.tile([P, J], F32, name="b_first", tag=f"b_first{t}", align_bytes=64)
+                if (branch, b, t) == (GATE, 0, 0):
+                    b_sb[branch, b, t] = keep.tile([P, J], F32, name="b_first", tag="b_first", align_bytes=64)
                 else:
                     b_sb[branch, b, t] = ring.tile([P, J], F32, name="b_sb", tag="b_sb", bufs=6)
                 on_scalar(b_sb[branch, b, t][:], bank[:])
@@ -292,7 +301,7 @@ def tile_list_intent_cell_step_kernel(
 
         h_stage = keep.tile([P, 16 * J], BF16, name="h_stage", align_bytes=64)
         h_woven = h_stage[:, 0 : 8 * J]
-        h_rows = h_stage[:, 8 * J : 16 * J].rearrange("p (u j) -> p u j", j=J)
+        h_rows = h_stage[:, 8 * J : 16 * J].rearrange("p (bt j) -> p bt j", j=J)
         h_codes = [keep.tile([P, J], U32, name=f"h_codes{b}", align_bytes=64) for b in range(2)]
         h_scales = [keep.tile([P, J], U8, name=f"h_scales{b}", align_bytes=64) for b in range(2)]
 
@@ -324,28 +333,28 @@ def tile_list_intent_cell_step_kernel(
 
         def finish(j0, copies):
             cols = slice(j0, j0 + HALF)
-            for m in range(N // P):
+            for out_tile in range(N // P):
                 bank = psum.tile([P, HALF], F32, name="bank_out", tag="bank")
                 for b in range(2):
-                    rows = slice(N * b + P * m, N * b + P * (m + 1))
+                    rows = slice(N * b + P * out_tile, N * b + P * (out_tile + 1))
                     nc.tensor.matmul_mx(
                         out=bank[:], lhsT=wo_codes[:, rows].bitcast(FP8X4), lhsT_scale=wo_scales[:, rows],
                         rhs=h_codes[b][:, cols].bitcast(FP8X4), rhs_scale=h_scales[b][:, cols],
                         start=(b == 0), stop=(b == 1),
                     )
                 result = ring.tile([P, HALF], F32, name="result", tag="result", bufs=6)
-                copies[m](result[:], bank[:])
-                nc.sync.dma_start(out[P * m : P * (m + 1), cols], result[:])
+                copies[out_tile](result[:], bank[:])
+                nc.sync.dma_start(out[P * out_tile : P * (out_tile + 1), cols], result[:])
 
         for tile in ROW_TILES[:AHEAD]:
             project_page(*tile)
         project_states(*ROW_TILES[0])
-        round_weight(on_vector, "wa1", 0, 1, after="wb1_raw")
+        round_weight(on_vector, "wb2", 0, 1, on_bytes_of="wb1_sc_raw")
 
         side_work = {
-            0: (lambda: None, lambda: quantize_weight("wa1", 0, 1)),
-            1: (lambda: round_weight(on_vector, "wb2", 0, 1, after="b_first0"), lambda: quantize_weight("wb2", 0, 1)),
-            2: (lambda: round_weight(on_vector, "wb2", 1, 1, after="b_first1"), lambda: quantize_weight("wb2", 1, 1)),
+            0: (lambda: None, lambda: quantize_weight("wa1", 0, 1, on_bytes_of="wb1_raw")),
+            1: (lambda: round_weight(on_vector, "wb2", 1, 1, on_bytes_of="b_first"), lambda: quantize_weight("wb2", 0, 1)),
+            2: (lambda: None, lambda: quantize_weight("wb2", 1, 1)),
             4: (lambda: round_wo(on_vector, 0), lambda: None),
             5: (lambda: weave_h(on_vector, 0, 0, J), lambda: quantize_h(0, 0, J)),
         }
@@ -365,19 +374,19 @@ def tile_list_intent_cell_step_kernel(
             activate(CAND, *tile, 0, J)
         project_states(*ROW_TILES[-1])
 
-        pieces = [(b, t, j0, HALF) for j0 in (0, HALF) for b, t in ROW_TILES[-2:]]
+        parts = [(b, t, j0, HALF) for j0 in (0, HALF) for b, t in ROW_TILES[-2:]]
         pending = whole_tiles[-1] + (0, J)
-        for n, piece in enumerate(pieces):
+        for nth, part in enumerate(parts):
             for branch in (GATE, CAND):
-                gather_add(branch, *piece)
-                activate(branch, *piece)
+                gather_add(branch, *part)
+                activate(branch, *part)
             product(*pending)
-            pending = piece
-            if n == 0:
+            pending = part
+            if nth == 0:
                 round_wo(on_scalar, 1)
-            if n == 1:
+            if nth == 1:
                 quantize_wo()
-            if n == 2:
+            if nth == 2:
                 weave_h(on_scalar, 1, 0, HALF)
         quantize_h(1, 0, HALF)
         product(*pending)

from contextlib import ExitStack

import concourse.mybir as mybir

H, N, T, T2, S, J = 1024, 384, 2048, 1024, 512, 512
FLOPS = 4697620480

F32 = mybir.dt.float32
BF16 = mybir.dt.bfloat16
I32 = mybir.dt.int32
U32 = mybir.dt.uint32
U16 = mybir.dt.uint16
U8 = mybir.dt.uint8
FP8X4 = mybir.dt.float8_e4m3fn_x4
FP4X4 = mybir.dt.float4_e2m1fn_x4
ACT = mybir.ActivationFunctionType
ALU = mybir.AluOpType

P = 128
PASS = 512
BANK = 512
GATE, CAND = 0, 1
ROW_TILES = [(b, t) for b in range(2) for t in range(4)]
AHEAD = 3
HALF = J // 2


def tile_list_intent_cell_step_kernel(
    tc, tab_words, tab_scales, offs, offs2, offs3, xs, base, wa1, wa2_words, wa2_scales,
    wb1_words, wb1_scales, wb2, gain, wo, out,
):
    nc = tc.nc
    on_scalar = nc.scalar.copy
    on_vector = nc.vector.tensor_copy

    def on_gpsimd(dst, src):
        for t in range(4):
            nc.gpsimd.tensor_scalar(
                dst[:, :, t].rearrange("p g i e -> p g e i"), src[:, :, t].rearrange("p g i e -> p g e i"),
                1.0, 0.0, ALU.mult, ALU.add,
            )

    with ExitStack() as ctx:
        keep = ctx.enter_context(tc.tile_pool(name="keep", bufs=1))
        ring = ctx.enter_context(tc.tile_pool(name="ring", bufs=2))
        psum = ctx.enter_context(tc.psum_pool(name="psum", bufs=8))

        idx = keep.tile([P, J // 16], U16, name="idx")
        idx2 = keep.tile([P, S // 16], U16, name="idx2")
        idx3 = keep.tile([P, J // 16], U16, name="idx3")

        tab_sc = keep.tile([P, 2, T], U8, name="tab_sc", tag="tab_sc", align_bytes=64)
        wa2_sc_raw = keep.tile([P, 1, H], U8, name="wa2_sc_raw", align_bytes=64)
        wb1_sc_raw = keep.tile([P, 2, H], U8, name="wb1_sc_raw", tag="wb1_sc_raw", align_bytes=64)
        for plane in (wa2_sc_raw, tab_sc, wb1_sc_raw):
            nc.vector.memset(plane[:].rearrange("p a c -> p (a c)").bitcast(I32), 0)

        warm = keep.tile([P, 2], F32, name="warm")
        nc.vector.memset(warm[:, 0:1], 0.0)
        nc.scalar.activation(warm[:, 1:2], warm[:, 0:1], ACT.Sigmoid)

        def load_scales(plane, src):
            for quad in range(4):
                nc.sync.dma_start(
                    plane[32 * quad : 32 * quad + 4].bitcast(I32),
                    src[:, 4 * quad : 4 * quad + 4, :].rearrange("a r c -> r a c").bitcast(I32),
                )

        base_rows = base.rearrange("(p i) t -> i p t", i=4)
        xs_rows = xs.rearrange("(p i) t -> i p t", i=4)
        page = [keep.tile([P, T2], F32, name=f"page{i}", align_bytes=64) for i in range(4)]
        frames = [keep.tile([P, S], F32, name=f"frames{i}", tag=f"frames{i}", align_bytes=64) for i in range(4)]

        def load_page_rows(i):
            nc.sync.dma_start(page[i][:], base_rows[i])
            nc.sync.dma_start(frames[i][:], xs_rows[i])

        raw = {}

        def streamed(columns):
            return ring.tile([P, 4, columns], F32, name="raw", tag="raw", bufs=4)

        def load_weight(name, w, a, b, dst):
            rows = w[PASS * a : PASS * (a + 1), PASS * b : PASS * (b + 1)]
            raw[name, a, b] = dst
            nc.sync.dma_start(dst[:], rows.rearrange("(p i) c -> p i c", i=4))

        def load_wo(b):
            rows = wo[PASS * b : PASS * (b + 1), :].rearrange("(g t e) n -> e g t n", t=4, e=4)
            raw["wo", b] = streamed(N)
            for e in range(4):
                nc.sync.dma_start(raw["wo", b][e:P:4], rows[e])

        tab_w = [keep.tile([P, T], I32, name=f"tab_w{a}", tag=f"tab_w{a}", align_bytes=64) for a in range(2)]

        def load_table_words(a):
            nc.sync.dma_start(tab_w[a][:], tab_words[a].rearrange("p t i -> p (t i)").bitcast(I32))

        wa2_raw = keep.tile([P, H], I32, name="wa2_raw")
        wb1_raw = keep.tile([P, 2, H // 2], I32, name="wb1_raw", tag="wb1_raw", align_bytes=64)

        gain_sb = keep.tile([P, 2, 16], F32, name="gain_sb")

        def load_gain():
            runs = gain.rearrange("(b g x) -> g b x", b=2, x=16)
            for e in range(4):
                nc.sync.dma_start(gain_sb[e:P:4, :, 0:13], runs[:, :, e : e + 13])

        def quantize(codes, scales, src):
            nc.vector.quantize_mx(out=codes.bitcast(FP8X4), scales=scales, in_=src)

        def weave(copy, dst, src):
            copy(dst.rearrange("p (c e i) -> p c i e", e=4, i=4), src.rearrange("p i (c e) -> p c i e", e=4))

        woven = {}
        quantized = {}

        def round_weight(copy, name, a, b, on_bytes_of=None):
            dst = keep.tile([P, 4 * PASS], BF16, name="woven", tag=on_bytes_of or f"woven_{name}{a}{b}", align_bytes=64)
            copy(
                dst[:].rearrange("p (t g e i) -> p g t i e", t=4, e=4, i=4),
                raw[name, a, b][:].rearrange("p i (g t e) -> p g t i e", t=4, e=4),
            )
            woven[name, a, b] = dst

        def quantize_weight(name, a, b, on_bytes_of=""):
            codes = keep.tile([P, PASS], U32, name=f"{name}_codes{a}{b}", tag=on_bytes_of, align_bytes=64)
            scales = keep.tile([P, PASS], U8, name=f"{name}_scales{a}{b}", align_bytes=64)
            quantize(codes[:], scales[:], woven[name, a, b][:])
            quantized[name, a, b] = (codes, scales)

        page_woven = [
            keep.tile([P, 4 * BANK], BF16, name=f"page_woven{c}", tag=f"page_woven{c}", align_bytes=64)
            for c in range(2)
        ]
        page_codes = keep.tile([P, T2], U32, name="page_codes", align_bytes=64)
        page_scales = keep.tile([P, T2], U8, name="page_scales", align_bytes=64)

        def scatter(i):
            nc.vector.tensor_copy(page[i][:].indirect(idx2[:]), frames[i][:])

        def quantize_page(c):
            cols = slice(BANK * c, BANK * (c + 1))
            quantize(page_codes[:, cols], page_scales[:, cols], page_woven[c][:])

        wa2_codes = keep.tile([P, H], U32, name="wa2_codes", align_bytes=64)
        wa2_sc = keep.tile([P, H], U8, name="wa2_sc", align_bytes=64)

        def order_wa2_words():
            nc.vector.tensor_copy(
                wa2_codes[:].bitcast(I32).rearrange("p (b t g e) -> p b t g e", b=2, t=4, e=4),
                wa2_raw[:].rearrange("p (b g t e) -> p b t g e", b=2, t=4, e=4),
            )

        def order_wa2_scales():
            nc.vector.tensor_copy(
                wa2_sc[:].bitcast(I32).rearrange("p (b t g) -> p b t g", b=2, t=4),
                wa2_sc_raw[:, 0, :].bitcast(I32).rearrange("p (b g t) -> p b t g", b=2, t=4),
            )

        def order_wb1():
            codes = keep.tile([P, 2, 2 * H], U8, name="wb1_codes", tag="tab_w1", align_bytes=64)
            scales = keep.tile([P, 2, H], U8, name="wb1_sc", tag="tab_sc", align_bytes=64)
            as_words = "p a c -> p (a c)"
            nc.vector.tensor_copy(
                codes[:].rearrange(as_words).bitcast(I32).rearrange("p (u t g w) -> p u t g w", u=4, t=4, w=2),
                wb1_raw[:].rearrange("p a (b g t w) -> p (a b) t g w", b=2, t=4, w=2),
            )
            nc.vector.tensor_copy(
                scales[:].rearrange(as_words).bitcast(I32).rearrange("p (u t g) -> p u t g", u=4, t=4),
                wb1_sc_raw[:].rearrange(as_words).bitcast(I32).rearrange("p (u g t) -> p u t g", u=4, t=4),
            )
            return codes, scales

        def gather_table():
            codes = keep.tile([P, 2 * J], U32, name="v_codes", tag="page_woven1", align_bytes=64)
            for a in range(2):
                nc.vector.tensor_copy(codes[:, J * a : J * (a + 1)], tab_w[a][:].bitcast(U32).indirect(idx[:]))
            scales = keep.tile([P, 2 * J], U8, name="v_scales", tag="tab_w0", align_bytes=64)
            for a in range(2):
                nc.vector.tensor_copy(scales[:, J * a : J * (a + 1)], tab_sc[:, a, :].indirect(idx[:]))
            return codes, scales

        with tc.tile_pool(name="staging", bufs=1) as staging:
            stretch = 2 * 4 * PASS
            stage = staging.tile([P, 4 * stretch + BANK], BF16, name="stage", align_bytes=64)
            page_rows = stage[:, 0 : 4 * stretch].rearrange("p (i c) -> p i c", i=4)[:, :, 0:T2]

            def staged(start):
                return stage[:, start : start + stretch].bitcast(F32).rearrange("p (i c) -> p i c", i=4)

            nc.sync.dma_start(idx2[:], offs2)
            load_page_rows(0)
            load_page_rows(1)
            load_weight("wa1", wa1, 0, 0, staged(stretch))
            load_page_rows(2)
            load_weight("wb2", wb2, 0, 0, staged(2 * stretch))
            load_page_rows(3)
            load_weight("wb2", wb2, 1, 0, staged(3 * stretch + BANK))
            load_scales(wa2_sc_raw, wa2_scales)
            nc.sync.dma_start(wa2_raw[:], wa2_words[0].rearrange("p c i -> p (c i)").bitcast(I32))
            nc.sync.dma_start(idx[:], offs)
            load_scales(tab_sc, tab_scales)
            load_table_words(0)
            load_weight("wa1", wa1, 0, 1, streamed(PASS))
            load_table_words(1)
            nc.sync.dma_start(idx3[:], offs3)
            load_scales(wb1_sc_raw, wb1_scales)
            nc.sync.dma_start(wb1_raw[:], wb1_words.rearrange("a p c -> p a c").bitcast(I32))
            load_weight("wb2", wb2, 0, 1, streamed(PASS))
            load_gain()
            load_weight("wb2", wb2, 1, 1, streamed(PASS))
            load_wo(0)
            load_wo(1)

            for i, weight_piece in enumerate((("wa1", 0, 0), ("wb2", 0, 0), ("wb2", 1, 0))):
                scatter(i)
                on_scalar(page_rows[:, i, :], page[i][:])
                round_weight(on_scalar, *weight_piece)
            scatter(3)
            halves = ((on_vector, slice(0, BANK)), (on_scalar, slice(BANK, T2)))
            for copy, cols in halves:
                copy(page_rows[:, 3, cols], page[3][:, cols])
            quantize_weight("wa1", 0, 0, on_bytes_of="frames3")
            for c, (copy, cols) in enumerate(halves):
                weave(copy, page_woven[c][:], page_rows[:, :, cols])

        products = ctx.enter_context(tc.tile_pool(name="products", bufs=2 * (AHEAD + 1)))

        order_wa2_scales()
        quantize_page(0)
        order_wa2_words()
        quantize_weight("wb2", 0, 0, on_bytes_of="page_woven0")
        quantize_page(1)
        quantize_weight("wb2", 1, 0)
        round_weight(on_gpsimd, "wa1", 0, 1, on_bytes_of="woven_wb210")
        v_codes, v_scales = gather_table()
        wb1_codes, wb1_sc = order_wb1()

        a_sb = {}
        b_sb = {}
        sums = {}
        acts = {}

        def project_page(b, t):
            for branch in (GATE, CAND):
                if branch == GATE:
                    codes, scales = quantized["wa1", 0, b]
                    rows = slice(P * t, P * (t + 1))
                else:
                    codes, scales = wa2_codes, wa2_sc
                    rows = slice(PASS * b + P * t, PASS * b + P * (t + 1))
                full = products.tile([P, T2], F32, name="a_full")
                for c in range(2):
                    cols = slice(BANK * c, BANK * (c + 1))
                    bank = psum.tile([P, BANK], F32, name="bank_a", tag="bank")
                    nc.tensor.matmul_mx(
                        out=bank[:], lhsT=codes[:, rows].bitcast(FP8X4), lhsT_scale=scales[:, rows],
                        rhs=page_codes[:, cols].bitcast(FP8X4), rhs_scale=page_scales[:, cols],
                        start=True, stop=True,
                    )
                    on_scalar(full[:, cols], bank[:])
                a_sb[branch, b, t] = full

        def project_states(b, t):
            for branch in (GATE, CAND):
                bank = psum.tile([P, BANK], F32, name="bank_b", tag="bank")
                for a in range(2):
                    if branch == GATE:
                        first = PASS * b + P * t
                        lhs = wb1_codes[:, a, 2 * first : 2 * (first + P)].bitcast(FP4X4)
                        lhs_scale = wb1_sc[:, a, first : first + P]
                    else:
                        codes, scales = quantized["wb2", a, b]
                        lhs = codes[:, P * t : P * (t + 1)].bitcast(FP8X4)
                        lhs_scale = scales[:, P * t : P * (t + 1)]
                    picked = slice(J * a, J * (a + 1))
                    nc.tensor.matmul_mx(
                        out=bank[:], lhsT=lhs, lhsT_scale=lhs_scale,
                        rhs=v_codes[:, picked].bitcast(FP8X4), rhs_scale=v_scales[:, picked],
                        start=(a == 0), stop=(a == 1),
                    )
                if (branch, b, t) == (GATE, 0, 0):
                    b_sb[branch, b, t] = keep.tile([P, J], F32, name="b_first", tag="b_first", align_bytes=64)
                else:
                    b_sb[branch, b, t] = ring.tile([P, J], F32, name="b_sb", tag="b_sb", bufs=6)
                on_scalar(b_sb[branch, b, t][:], bank[:])

        def gather_add(branch, b, t, j0, width):
            total = ring.tile([P, width], F32, name="total", tag="total", bufs=4)
            nc.vector.tensor_tensor(
                total[:], a_sb[branch, b, t][:].indirect(idx3[:, j0 // 16 : (j0 + width) // 16]),
                b_sb[branch, b, t][:, j0 : j0 + width], ALU.add,
            )
            sums[branch, b, t, j0] = total

        def activate(branch, b, t, j0, width):
            value = ring.tile([P, width], F32, name="act", tag="act", bufs=4)
            nc.scalar.activation(value[:], sums[branch, b, t, j0][:], ACT.Sigmoid if branch == GATE else ACT.Tanh)
            acts[branch, b, t, j0] = value

        h_stage = keep.tile([P, 16 * J], BF16, name="h_stage", align_bytes=64)
        h_woven = h_stage[:, 0 : 8 * J]
        h_rows = h_stage[:, 8 * J : 16 * J].rearrange("p (bt j) -> p bt j", j=J)
        h_codes = [keep.tile([P, J], U32, name=f"h_codes{b}", align_bytes=64) for b in range(2)]
        h_scales = [keep.tile([P, J], U8, name=f"h_scales{b}", align_bytes=64) for b in range(2)]

        def product(b, t, j0, width):
            nc.vector.scalar_tensor_tensor(
                h_rows[:, 4 * b + t, j0 : j0 + width], acts[GATE, b, t, j0][:], gain_sb[:, b, 4 * t : 4 * t + 1],
                acts[CAND, b, t, j0][:], ALU.mult, ALU.mult,
            )

        def weave_h(copy, b, j0, width):
            start = 4 * (J * b + j0)
            weave(copy, h_woven[:, start : start + 4 * width], h_rows[:, 4 * b : 4 * (b + 1), j0 : j0 + width])

        def quantize_h(b, j0, width):
            start = 4 * (J * b + j0)
            cols = slice(j0, j0 + width)
            quantize(h_codes[b][:, cols], h_scales[b][:, cols], h_woven[:, start : start + 4 * width])

        wo_woven = keep.tile([P, 2 * 4 * N], BF16, name="wo_woven", tag="page_woven0", align_bytes=64)
        wo_codes = keep.tile([P, 2 * N], U32, name="wo_codes", align_bytes=64)
        wo_scales = keep.tile([P, 2 * N], U8, name="wo_scales", align_bytes=64)

        def round_wo(copy, b):
            weave(copy, wo_woven[:, 4 * N * b : 4 * N * (b + 1)], raw["wo", b][:])

        def quantize_wo():
            for cols in (slice(0, 512), slice(512, 2 * N)):
                quantize(wo_codes[:, cols], wo_scales[:, cols], wo_woven[:, 4 * cols.start : 4 * cols.stop])

        def finish(j0, copies):
            cols = slice(j0, j0 + HALF)
            for out_tile in range(N // P):
                bank = psum.tile([P, HALF], F32, name="bank_out", tag="bank")
                for b in range(2):
                    rows = slice(N * b + P * out_tile, N * b + P * (out_tile + 1))
                    nc.tensor.matmul_mx(
                        out=bank[:], lhsT=wo_codes[:, rows].bitcast(FP8X4), lhsT_scale=wo_scales[:, rows],
                        rhs=h_codes[b][:, cols].bitcast(FP8X4), rhs_scale=h_scales[b][:, cols],
                        start=(b == 0), stop=(b == 1),
                    )
                result = ring.tile([P, HALF], F32, name="result", tag="result", bufs=6)
                copies[out_tile](result[:], bank[:])
                nc.sync.dma_start(out[P * out_tile : P * (out_tile + 1), cols], result[:])

        for tile in ROW_TILES[:AHEAD]:
            project_page(*tile)
        project_states(*ROW_TILES[0])
        round_weight(on_vector, "wb2", 0, 1, on_bytes_of="wb1_sc_raw")

        side_work = {
            0: (lambda: None, lambda: quantize_weight("wa1", 0, 1, on_bytes_of="wb1_raw")),
            1: (lambda: round_weight(on_vector, "wb2", 1, 1, on_bytes_of="b_first"), lambda: quantize_weight("wb2", 0, 1)),
            2: (lambda: None, lambda: quantize_weight("wb2", 1, 1)),
            4: (lambda: round_wo(on_vector, 0), lambda: None),
            5: (lambda: weave_h(on_vector, 0, 0, J), lambda: quantize_h(0, 0, J)),
        }
        whole_tiles = ROW_TILES[:-2]
        for step, tile in enumerate(whole_tiles):
            before, after = side_work.get(step, (lambda: None, lambda: None))
            before()
            gather_add(GATE, *tile, 0, J)
            after()
            project_states(*ROW_TILES[step + 1])
            if step + AHEAD < len(ROW_TILES):
                project_page(*ROW_TILES[step + AHEAD])
            gather_add(CAND, *tile, 0, J)
            if step > 0:
                product(*whole_tiles[step - 1], 0, J)
            activate(GATE, *tile, 0, J)
            activate(CAND, *tile, 0, J)
        project_states(*ROW_TILES[-1])

        parts = [(b, t, j0, HALF) for j0 in (0, HALF) for b, t in ROW_TILES[-2:]]
        pending = whole_tiles[-1] + (0, J)
        for nth, part in enumerate(parts):
            for branch in (GATE, CAND):
                gather_add(branch, *part)
                activate(branch, *part)
            product(*pending)
            pending = part
            if nth == 0:
                round_wo(on_scalar, 1)
            if nth == 1:
                quantize_wo()
            if nth == 2:
                weave_h(on_scalar, 1, 0, HALF)
        quantize_h(1, 0, HALF)
        product(*pending)
        finish(0, (on_scalar, on_scalar, on_scalar))
        weave_h(on_vector, 1, HALF, HALF)
        quantize_h(1, HALF, HALF)
        finish(HALF, (on_scalar, on_vector, on_scalar))
